import numpy as np
import ml_dtypes


def mxq(x, axis, fmt="e4m3"):
    dtype, down = {"e4m3": (ml_dtypes.float8_e4m3fn, 7), "e5m2": (ml_dtypes.float8_e5m2, 14)}[fmt]
    v = np.moveaxis(np.asarray(x, np.float32).astype(ml_dtypes.bfloat16).astype(np.float64), axis, -1)
    blocks = v.reshape(v.shape[:-1] + (-1, 32))
    amax = np.abs(blocks).max(-1, keepdims=True)
    byte = np.maximum(np.where(amax > 0, np.frexp(amax)[1] - 1 + 127, 0) - down, 1)
    scale = np.exp2(byte - 127.0)
    codes = (blocks / scale).astype(np.float32).astype(dtype).astype(np.float64)
    return np.moveaxis((codes * scale).reshape(v.shape), -1, axis)


WIDE = False


def mx_kscale(k):
    if not WIDE:
        return np.ones(k)
    levels = np.array([10, -10, 5, -5, 0])
    if k % 512:
        return np.exp2(np.random.permutation(np.resize(levels, k // 32))).repeat(32)
    a = np.empty((k // 512, 16))
    for p in range(k // 512):
        a[p, :8] = np.random.permutation(np.resize(levels, 8))
        for g in range(8):
            far = levels[np.abs(levels - a[p, g]) >= 10]
            a[p, g + 8] = far[np.random.randint(len(far))]
    return np.exp2(a.ravel()).repeat(32)


BF16 = ml_dtypes.bfloat16


def bf(x):
    return np.asarray(x, np.float32).astype(BF16)


def f64(x):
    return np.asarray(x).astype(np.float64)


E2M1 = np.array([0.0, 0.5, 1.0, 1.5, 2.0, 3.0, 4.0, 6.0, -0.0, -0.5, -1.0, -1.5, -2.0, -3.0, -4.0, -6.0])


def pack_weight(w, fmt):
    k, n = w.shape
    w = f64(bf(w)).reshape(k // 32, 32, n)
    amax = np.abs(w).max(1)
    if fmt == "e4m3":
        byte = np.frexp(amax)[1] - 1 + 127 - 7
    else:
        mant, ex = np.frexp(amax / 6.0)
        byte = np.where(mant > 0.5, ex, ex - 1) + 127
    byte = np.clip(np.where(amax > 0, byte, 1), 1, 254)
    scaled = (w * np.exp2(127.0 - byte)[:, None, :]).reshape(k, n).astype(np.float32)
    by_word = np.ascontiguousarray(scaled.reshape(k // 512, 128, 4, n).transpose(0, 1, 3, 2))
    if fmt == "e4m3":
        words = by_word.astype(ml_dtypes.float8_e4m3fn).view(np.uint8)
    else:
        c = by_word.astype(ml_dtypes.float4_e2m1fn).view(np.uint8) & 0xF
        words = c[..., 0::2] | (c[..., 1::2] << 4)
    return np.ascontiguousarray(words), np.ascontiguousarray(byte.astype(np.uint8).reshape(k // 512, 16, n))


def unpack_weight(words, scales, fmt):
    g, p, n, _ = words.shape
    if fmt == "e4m3":
        vals = np.ascontiguousarray(words).view(ml_dtypes.float8_e4m3fn).astype(np.float64)
    else:
        nib = np.empty((g, p, n, 4), np.uint8)
        nib[..., 0::2] = words & 0xF
        nib[..., 1::2] = words >> 4
        vals = E2M1[nib]
    vals = vals * np.repeat(np.exp2(scales.astype(np.float64) - 127.0), 8, axis=1)[..., None]
    return vals.transpose(0, 1, 3, 2).reshape(g * 512, n)
def pack4(w):
    words, scales = pack_weight(w, "e2m1")
    return words.reshape(words.shape[0], 128, -1), scales


def unpack4(words, scales):
    return unpack_weight(words.reshape(words.shape[0], 128, -1, 2), scales, "e2m1")


M, K, N, R, T = 1024, 1024, 1024, 512, 2


def setup_inputs():
    s, r = mx_kscale(K), mx_kscale(R)
    x = bf(np.random.standard_normal((M, K)) / np.sqrt(K) * s)
    w_words, w_scales = pack_weight(np.random.standard_normal((K, N)) / s[:, None], "e4m3")
    u_words, u_scales = pack4(np.random.standard_normal((R, T * K)) * r[:, None] / np.tile(s, T))
    v_words, v_scales = pack4(np.random.standard_normal((R, T * N)) / np.sqrt(R) / r[:, None])
    return {"x": x,
            "w_words": w_words, "w_scales": w_scales,
            "u_words": u_words, "u_scales": u_scales,
            "v_words": v_words, "v_scales": v_scales,
            "lim": bf(np.random.uniform(0.5, 1.5, (T, K)) / s),
            "lam": bf(np.random.uniform(0.3, 1.0, (M, T)))}


def reference(x, w_words, w_scales, u_words, u_scales, v_words, v_scales, lim, lam):
    w = unpack_weight(w_words, w_scales, "e4m3")
    u = unpack4(u_words, u_scales)
    v = unpack4(v_words, v_scales)
    lim, lam = f64(lim), f64(lam)
    xq = mxq(f64(x), 1, "e4m3")
    y = xq @ w
    for i in range(T):
        d = u[:, i * K:(i + 1) * K].T @ v[:, i * N:(i + 1) * N]
        c = np.minimum(np.maximum(d, -lim[i][:, None]), lim[i][:, None])
        z = xq @ mxq(c, 0, "e4m3")
        y = y + lam[:, i][:, None] * z
    return y

@@ -1,0 +1,328 @@
+from contextlib import ExitStack
+
+import concourse.mybir as mybir
+from concourse.masks import make_identity
+
+M, K, N, R, T = 1024, 1024, 1024, 512, 2
+
+F32 = mybir.dt.float32
+BF16 = mybir.dt.bfloat16
+I32 = mybir.dt.int32
+U32 = mybir.dt.uint32
+U8 = mybir.dt.uint8
+E4M3 = mybir.dt.float8_e4m3fn_x4
+E2M1 = mybir.dt.float4_e2m1fn_x4
+ALU = mybir.AluOpType
+ACT = mybir.ActivationFunctionType
+
+FLOPS = 2 * M * K * N * (1 + T) + 2 * T * R * K * N
+
+P = 128
+NH = 512
+MT = M // P
+G = K // 512
+H = N // NH
+VCS = (512, 512, 512, 256, 224, 224, 192, 128)
+ONV = ((), (1, 2), (), (1, 2), (), (), (), ())
+POS = 4
+GCL = ()
+WARM = 24
+SG = ()
+YS = (1, 2, 1, 2, 2, 0, 0, 0)
+
+
+def tile_clipped_task_arithmetic_s4_kernel(
+    tc, x, w_words, w_scales, u_words, u_scales, v_words, v_scales, lim, lam, out
+):
+    nc = tc.nc
+    with ExitStack() as ctx:
+        keep = ctx.enter_context(tc.tile_pool(name="keep", bufs=1))
+        work = ctx.enter_context(tc.tile_pool(name="work", bufs=4))
+        psum_d = ctx.enter_context(tc.psum_pool(name="psum_d", bufs=4))
+        psum_z = ctx.enter_context(tc.psum_pool(name="psum_z", bufs=4))
+        ctx.enter_context(tc.manual_schedule())
+
+        u_raw = [keep.tile([P, 2 * K], U8, name=f"u_raw{i}", align_bytes=64) for i in range(T)]
+        u_ord = [keep.tile([P, G, 4, P, 2], U8, name=f"u_ord{i}", align_bytes=64) for i in range(T)]
+        us_raw = keep.tile([P, T * K], U8, name="us_raw", align_bytes=64)
+        us_ord = [keep.tile([P, G, 4, P], U8, name=f"us_ord{i}", align_bytes=64) for i in range(T)]
+        v_sb = [[keep.tile([P, 2 * NH], U8, name=f"v{i}_{h}", align_bytes=64) for h in range(H)] for i in range(T)]
+        vs_sb = keep.tile([P, T * N], U8, name="vs_sb", align_bytes=64)
+        w_sb = [keep.tile([P, N * 4], U8, name=f"w{g}", align_bytes=64) for g in range(G)]
+        ws_sb = keep.tile([P, G, N], U8, name="ws_sb", align_bytes=64)
+        x_sb = [keep.tile([P, 2, K], BF16, name=f"x{c}", align_bytes=64) for c in range(MT // 2)]
+        xq = [keep.tile([P, 4, P], U32, name=f"xq{c}", align_bytes=64) for c in range(MT // 2)]
+        xs = [keep.tile([P, 4, P], U8, name=f"xs{c}", align_bytes=64) for c in range(MT // 2)]
+        cq = [keep.tile([P, NH], U32, name=f"cq{j}", align_bytes=64) for j in range(8)]
+        cs = [keep.tile([P, NH], U8, name=f"cs{j}", align_bytes=64) for j in range(8)]
+        acc = [[keep.tile([P, NH], F32, name=f"acc{h}_{m}", align_bytes=64) for m in range(MT)] for h in range(H)]
+        warm = keep.tile([P, 4 * P], BF16, name="warm", align_bytes=64)
+        warm_q = keep.tile([P, P], U32, name="warm_q", align_bytes=64)
+        warm_s = keep.tile([P, P], U8, name="warm_s", align_bytes=64)
+        act_dummy = keep.tile([P, 1], F32, name="act_dummy")
+        ident = keep.tile([P, P], F32, name="ident")
+        lim_bf = keep.tile([P, T, G, 4], BF16, name="lim_bf")
+        lim_hi = keep.tile([P, T * G * 4], F32, name="lim_hi")
+        lim_lo = keep.tile([P, T * G * 4], F32, name="lim_lo")
+        lam_bf = keep.tile([P, MT * T], BF16, name="lam_bf")
+        lam_f = keep.tile([P, MT * T], F32, name="lam_f")
+
+        def load_u(i, eng):
+            eng.dma_start(out=u_raw[i][:].bitcast(I32), in_=u_words[0, :, 2 * K * i : 2 * K * (i + 1)].bitcast(I32))
+
+        def load_v(i, h, eng):
+            c0 = 2 * (N * i + NH * h)
+            eng.dma_start(out=v_sb[i][h][:].bitcast(I32), in_=v_words[0, :, c0 : c0 + 2 * NH].bitcast(I32))
+
+        def load_scales(dst, rows, engines):
+            for q in range(4):
+                engines[q].dma_start(out=dst[32 * q : 32 * q + 4, :].bitcast(I32), in_=rows[4 * q : 4 * q + 4, :].bitcast(I32))
+
+        nc.vector.memset(us_raw[:].bitcast(I32), 0)
+        nc.vector.memset(vs_sb[:].bitcast(I32), 0)
+        nc.vector.memset(warm[:].bitcast(I32), 0)
+        x_view = x.rearrange("(p c m) k -> c p m k", c=MT // 2, m=2)
+
+        def load_x(c):
+            nc.sync.dma_start(out=x_sb[c][:], in_=x_view[c])
+
+        def load_w(g):
+            nc.sync.dma_start(out=w_sb[g][:].bitcast(I32), in_=w_words[g].rearrange("p n t -> p (n t)").bitcast(I32))
+
+        nc.gpsimd.memset(ws_sb[:].rearrange("p g n -> p (g n)").bitcast(I32), 0)
+        nc.gpsimd.dma_start(out=lim_bf[:], in_=lim.rearrange("i (g p t) -> p i g t", g=G, t=4))
+        make_identity(nc, ident[:])
+        load_u(0, nc.sync)
+        load_v(0, 0, nc.sync)
+        for q in range(4):
+            nc.sync.dma_start(out=us_raw[32 * q : 32 * q + 4, :].bitcast(I32), in_=u_scales[0, 4 * q : 4 * q + 4, :].bitcast(I32))
+        for q in range(4):
+            nc.scalar.dma_start(out=vs_sb[32 * q : 32 * q + 4, :].bitcast(I32), in_=v_scales[0, 4 * q : 4 * q + 4, :].bitcast(I32))
+        load_x(0)
+        load_x(1)
+        load_u(1, nc.sync)
+        load_v(1, 0, nc.sync)
+        load_x(2)
+        load_x(3)
+        for q in range(4):
+            nc.sync.dma_start(
+                out=ws_sb[32 * q : 32 * q + 4, :, :].bitcast(I32),
+                in_=w_scales[:, 4 * q : 4 * q + 4, :].rearrange("g r n -> r g n").bitcast(I32),
+            )
+        load_w(0)
+        load_w(1)
+        nc.sync.dma_start(out=lam_bf[:], in_=lam.rearrange("(p m) i -> p (m i)", m=MT))
+        load_v(0, 1, nc.sync)
+        load_v(1, 1, nc.sync)
+
+        nc.gpsimd.tensor_copy(out=lam_f[:], in_=lam_bf[:])
+
+        units = [(h, i, g) for h in range(H) for i in range(T) for g in range(G)]
+
+        def order_u(i, g, eng):
+            eng.tensor_copy(
+                out=u_ord[i][:, g, :, :, :],
+                in_=u_raw[i][:, 1024 * g : 1024 * (g + 1)].rearrange("p (m t b) -> p t m b", t=4, b=2),
+            )
+            eng.tensor_copy(
+                out=us_ord[i][:, g, :, :],
+                in_=us_raw[:, K * i + 512 * g : K * i + 512 * (g + 1)].rearrange("p (m t) -> p t m", t=4),
+            )
+
+        d_sb = {}
+        grp = {}
+
+        def task_vectors(j, on_vector=(), ts=range(4)):
+            h, i, g = units[j]
+            if j not in d_sb:
+                d_sb[j] = work.tile([P, 4, NH], BF16, name="d_sb", align_bytes=64)
+            for t in ts:
+                ps = psum_d.tile([P, NH], F32, name="ps_d")
+                nc.tensor.matmul_mx(
+                    out=ps[:],
+                    lhsT=u_ord[i][:, g, t, :, :].rearrange("p m b -> p (m b)").bitcast(E2M1),
+                    lhsT_scale=us_ord[i][:, g, t, :],
+                    rhs=v_sb[i][h][:].bitcast(E2M1),
+                    rhs_scale=vs_sb[:, N * i + NH * h : N * i + NH * (h + 1)],
+                    start=True,
+                    stop=True,
+                )
+                if t in on_vector:
+                    clip(j, t, ps[:])
+                else:
+                    nc.scalar.copy(out=d_sb[j][:, t, :], in_=ps[:])
+
+        def clip(j, t, src):
+            h, i, g = units[j]
+            c = (i * G + g) * 4 + t
+            eng = nc.gpsimd if (j, t) in GCL else nc.vector
+            eng.tensor_scalar(
+                out=d_sb[j][:, t, :], in0=src, scalar1=lim_hi[:, c : c + 1], scalar2=lim_lo[:, c : c + 1], op0=ALU.min, op1=ALU.max
+            )
+
+        def clip_rest(j, on_vector):
+            for t in range(4):
+                if t not in on_vector:
+                    clip(j, t, d_sb[j][:, t, :])
+
+        def interleave(j, cols, scalar_cols):
+            grp[j] = work.tile([P, NH, 4], BF16, name="grp", align_bytes=64)
+            if cols > 0:
+                nc.vector.tensor_copy(
+                    out=grp[j][:, 0:cols, :].rearrange("p (c i) t -> p c t i", i=4), in_=d_sb[j][:, :, 0:cols].rearrange("p t (c i) -> p c t i", i=4)
+                )
+            if scalar_cols:
+                nc.scalar.copy(
+                    out=grp[j][:, cols:NH, :].rearrange("p (c i) t -> p c t i", i=4), in_=d_sb[j][:, :, cols:NH].rearrange("p t (c i) -> p c t i", i=4)
+                )
+
+        def quantize(j):
+            nc.vector.quantize_mx(out=cq[j][:].bitcast(E4M3), scales=cs[j][:], in_=grp[j][:].rearrange("p n t -> p (n t)"))
+
+        xg = {}
+
+        def turn_x(m):
+            c, mm = divmod(m, 2)
+            if mm == 0:
+                xg[c] = work.tile([P, 4, P, 4], BF16, name="xg", align_bytes=64)
+            ps = psum_z.tile([P, G, 2, P], F32, name="ps_z")
+            words = x_sb[c][:, mm, :].bitcast(F32)
+            for g in range(G):
+                for u in range(2):
+                    nc.tensor.transpose(ps[:, g, u, :], words[:, 256 * g + u : 256 * (g + 1) : 2], ident[:])
+            nc.scalar.copy(
+                out=xg[c][:, 2 * mm : 2 * mm + 2, :, :].bitcast(F32),
+                in_=ps[:].rearrange("p g u n -> p g n u"),
+            )
+
+        def quantize_x(c):
+            nc.vector.quantize_mx(
+                out=xq[c][:].rearrange("p a n -> p (a n)").bitcast(E4M3),
+                scales=xs[c][:].rearrange("p a n -> p (a n)"),
+                in_=xg[c][:].rearrange("p a n t -> p (a n t)"),
+            )
+
+        def x_times(m, rhs, rhs_scale, cols=slice(0, NH)):
+            c, mm = divmod(m, 2)
+            ps = psum_z.tile([P, NH], F32, name="ps_z")
+            for g in range(G):
+                nc.tensor.matmul_mx(
+                    out=ps[:, cols],
+                    lhsT=xq[c][:, 2 * mm + g, :].bitcast(E4M3),
+                    lhsT_scale=xs[c][:, 2 * mm + g, :],
+                    rhs=rhs[g][:, cols].bitcast(E4M3),
+                    rhs_scale=rhs_scale[g][:, cols],
+                    start=(g == 0),
+                    stop=(g == G - 1),
+                )
+            return ps
+
+        def base(h, m):
+            ps = x_times(
+                m,
+                [w_sb[g][:].bitcast(U32)[:, NH * h : NH * (h + 1)] for g in range(G)],
+                [ws_sb[:, g, NH * h : NH * (h + 1)] for g in range(G)],
+            )
+            nc.scalar.copy(out=acc[h][m][:], in_=ps[:])
+
+        out_view = out.rearrange("(p m) n -> m p n", m=MT)
+
+        late = []
+
+        def task(pair, m, on_scalar=False, cols=slice(0, NH)):
+            h, i = divmod(pair, T)
+            ps = x_times(
+                m,
+                [cq[2 * pair + g] for g in range(G)],
+                [cs[2 * pair + g] for g in range(G)],
+                cols,
+            )
+            lam_col = lam_f[:, m * T + i : m * T + i + 1]
+            if on_scalar:
+                part = work.tile([P, NH], F32, name="part", align_bytes=64)
+                nc.scalar.activation(out=part[:], in_=ps[:], func=ACT.Copy, scale=lam_col)
+                nc.gpsimd.tensor_tensor(out=acc[h][m][:], in0=acc[h][m][:], in1=part[:], op=ALU.add)
+            else:
+                nc.vector.scalar_tensor_tensor(out=acc[h][m][:, cols], in0=ps[:, cols], scalar=lam_col, in1=acc[h][m][:, cols], op0=ALU.mult, op1=ALU.add)
+            if i == T - 1:
+                late.append((h, m, cols))
+                if not on_scalar:
+                    store(late.pop())
+                    if len(late) > 0 and m - late[0][1] >= 2:
+                        store(late.pop(0))
+
+        def store(hm):
+            h, m, cols = hm
+            nc.sync.dma_start(out=out_view[m][:, NH * h + cols.start : NH * h + cols.stop], in_=acc[h][m][:, cols])
+
+        nc.scalar.activation(out=act_dummy[:], in_=warm[:, 0:1], func=ACT.Copy, scale=1.0)
+        nc.vector.quantize_mx(out=warm_q[:].bitcast(E4M3), scales=warm_s[:], in_=warm[:])
+        ps_warm = psum_d.tile([P, NH], F32, name="ps_d")
+
+        def keep_warm(passes):
+            for r in range(passes):
+                nc.tensor.matmul_mx(
+                    out=ps_warm[:, 0:P], lhsT=warm_q[:].bitcast(E4M3), lhsT_scale=warm_s[:], rhs=warm_q[:].bitcast(E4M3), rhs_scale=warm_s[:], start=True, stop=True
+                )
+
+        keep_warm(WARM)
+        order_u(0, 0, nc.vector)
+        order_u(0, 1, nc.vector)
+        lim_cols = lim_bf[:].rearrange("p i g t -> p (i g t)")
+        nc.vector.tensor_copy(out=lim_hi[:], in_=lim_cols)
+        nc.vector.tensor_scalar(out=lim_lo[:], in0=lim_cols, scalar1=-1.0, scalar2=None, op0=ALU.mult)
+        order_u(1, 0, nc.vector)
+        order_u(1, 1, nc.vector)
+        task_vectors(0, ONV[0])
+        for m in range(0, 4):
+            turn_x(m)
+        task_vectors(1, ONV[1])
+        clip_rest(0, ONV[0])
+        clip_rest(1, ONV[1])
+        quantize_x(0)
+        interleave(0, VCS[0], VCS[0] < NH)
+        quantize_x(1)
+        quantize(0)
+        for m in range(4, 8):
+            turn_x(m)
+        interleave(1, VCS[1], VCS[1] < NH)
+        quantize_x(2)
+        quantize(1)
+        quantize_x(3)
+        task_vectors(2, ONV[2])
+        clip_rest(2, ONV[2])
+        base(0, 0)
+        interleave(2, VCS[2], VCS[2] < NH)
+        for m in range(1, 8):
+            if m == POS:
+                task_vectors(3, ONV[3])
+                quantize(2)
+            base(0, m)
+        ym = 0
+        for k in range(8):
+            pair, first = divmod(k, 2)
+            ms = range(4 * first, 4 * first + 4)
+            j = k + 3
+            if j < 8:
+                clip_rest(j, ONV[j])
+            task(pair, ms[0], (k, 0) in SG)
+            if j + 1 < 8:
+                task_vectors(j + 1, ONV[j + 1], (0, 1))
+            if j < 8:
+                interleave(j, VCS[j], VCS[j] < NH)
+            task(pair, ms[1], (k, 1) in SG)
+            if j + 1 < 8:
+                task_vectors(j + 1, ONV[j + 1], (2, 3))
+            task(pair, ms[2], (k, 2) in SG)
+            if j < 8:
+                quantize(j)
+            for r in range(YS[k]):
+                base(1, ym)
+                ym += 1
+            if k < 7:
+                task(pair, ms[3], (k, 3) in SG)
+            else:
+                task(pair, ms[3], cols=slice(0, NH // 2))
+                task(pair, ms[3], cols=slice(NH // 2, NH))
+        for hm in late:
+            store(hm)

@@ -9,11 +9,11 @@ F32 = mybir.dt.float32
 BF16 = mybir.dt.bfloat16
 I32 = mybir.dt.int32
 U32 = mybir.dt.uint32
+U16 = mybir.dt.uint16
 U8 = mybir.dt.uint8
 E4M3 = mybir.dt.float8_e4m3fn_x4
 E2M1 = mybir.dt.float4_e2m1fn_x4
 ALU = mybir.AluOpType
-ACT = mybir.ActivationFunctionType
 
 FLOPS = 2 * M * K * N * (1 + T) + 2 * T * R * K * N
 
@@ -22,13 +22,9 @@ NH = 512
 MT = M // P
 G = K // 512
 H = N // NH
-VCS = (512, 512, 512, 256, 224, 224, 192, 128)
-ONV = ((), (1, 2), (), (1, 2), (), (), (), ())
-POS = 4
-GCL = ()
-WARM = 24
-SG = ()
-YS = (1, 2, 1, 2, 2, 0, 0, 0)
+UNITS = H * T * G
+PIECE = 128
+GP_COLS = 384
 
 
 def tile_clipped_task_arithmetic_s4_kernel(
@@ -37,71 +33,66 @@ def tile_clipped_task_arithmetic_s4_kernel(
     nc = tc.nc
     with ExitStack() as ctx:
         keep = ctx.enter_context(tc.tile_pool(name="keep", bufs=1))
-        work = ctx.enter_context(tc.tile_pool(name="work", bufs=4))
-        psum_d = ctx.enter_context(tc.psum_pool(name="psum_d", bufs=4))
-        psum_z = ctx.enter_context(tc.psum_pool(name="psum_z", bufs=4))
+        work = ctx.enter_context(tc.tile_pool(name="work", bufs=3))
+        psum = ctx.enter_context(tc.psum_pool(name="psum", bufs=8))
         ctx.enter_context(tc.manual_schedule())
 
         u_raw = [keep.tile([P, 2 * K], U8, name=f"u_raw{i}", align_bytes=64) for i in range(T)]
-        u_ord = [keep.tile([P, G, 4, P, 2], U8, name=f"u_ord{i}", align_bytes=64) for i in range(T)]
+        u_ord = [[keep.tile([P, 4, 2 * P], U8, name=f"u_ord{i}_{g}", align_bytes=64) for g in range(G)] for i in range(T)]
         us_raw = keep.tile([P, T * K], U8, name="us_raw", align_bytes=64)
-        us_ord = [keep.tile([P, G, 4, P], U8, name=f"us_ord{i}", align_bytes=64) for i in range(T)]
+        us_ord = [[keep.tile([P, 4, P], U8, name=f"us_ord{i}_{g}", align_bytes=64) for g in range(G)] for i in range(T)]
         v_sb = [[keep.tile([P, 2 * NH], U8, name=f"v{i}_{h}", align_bytes=64) for h in range(H)] for i in range(T)]
         vs_sb = keep.tile([P, T * N], U8, name="vs_sb", align_bytes=64)
-        w_sb = [keep.tile([P, N * 4], U8, name=f"w{g}", align_bytes=64) for g in range(G)]
+        w_sb = [keep.tile([P, G, NH], I32, name=f"w{h}", align_bytes=64) for h in range(H)]
         ws_sb = keep.tile([P, G, N], U8, name="ws_sb", align_bytes=64)
         x_sb = [keep.tile([P, 2, K], BF16, name=f"x{c}", align_bytes=64) for c in range(MT // 2)]
         xq = [keep.tile([P, 4, P], U32, name=f"xq{c}", align_bytes=64) for c in range(MT // 2)]
         xs = [keep.tile([P, 4, P], U8, name=f"xs{c}", align_bytes=64) for c in range(MT // 2)]
-        cq = [keep.tile([P, NH], U32, name=f"cq{j}", align_bytes=64) for j in range(8)]
-        cs = [keep.tile([P, NH], U8, name=f"cs{j}", align_bytes=64) for j in range(8)]
+        cq = [keep.tile([P, NH], U32, name=f"cq{j}", align_bytes=64) for j in range(UNITS)]
+        cs = [keep.tile([P, NH], U8, name=f"cs{j}", align_bytes=64) for j in range(UNITS)]
         acc = [[keep.tile([P, NH], F32, name=f"acc{h}_{m}", align_bytes=64) for m in range(MT)] for h in range(H)]
-        warm = keep.tile([P, 4 * P], BF16, name="warm", align_bytes=64)
-        warm_q = keep.tile([P, P], U32, name="warm_q", align_bytes=64)
-        warm_s = keep.tile([P, P], U8, name="warm_s", align_bytes=64)
-        act_dummy = keep.tile([P, 1], F32, name="act_dummy")
         ident = keep.tile([P, P], F32, name="ident")
-        lim_bf = keep.tile([P, T, G, 4], BF16, name="lim_bf")
-        lim_hi = keep.tile([P, T * G * 4], F32, name="lim_hi")
-        lim_lo = keep.tile([P, T * G * 4], F32, name="lim_lo")
-        lam_bf = keep.tile([P, MT * T], BF16, name="lam_bf")
-        lam_f = keep.tile([P, MT * T], F32, name="lam_f")
+        lim_rows = keep.tile([P, 512], BF16, name="lim_rows")
+        lim_hi = keep.tile([P, T * G, 4], BF16, name="lim_hi")
+        lim_lo = keep.tile([P, T * G, 4], BF16, name="lim_lo")
+        lam_sb = keep.tile([P, MT * T], BF16, name="lam_sb")
 
-        def load_u(i, eng):
-            eng.dma_start(out=u_raw[i][:].bitcast(I32), in_=u_words[0, :, 2 * K * i : 2 * K * (i + 1)].bitcast(I32))
-
-        def load_v(i, h, eng):
-            c0 = 2 * (N * i + NH * h)
-            eng.dma_start(out=v_sb[i][h][:].bitcast(I32), in_=v_words[0, :, c0 : c0 + 2 * NH].bitcast(I32))
-
-        def load_scales(dst, rows, engines):
-            for q in range(4):
-                engines[q].dma_start(out=dst[32 * q : 32 * q + 4, :].bitcast(I32), in_=rows[4 * q : 4 * q + 4, :].bitcast(I32))
-
-        nc.vector.memset(us_raw[:].bitcast(I32), 0)
-        nc.vector.memset(vs_sb[:].bitcast(I32), 0)
-        nc.vector.memset(warm[:].bitcast(I32), 0)
         x_view = x.rearrange("(p c m) k -> c p m k", c=MT // 2, m=2)
+        out_view = out.rearrange("(p m) n -> m p n", m=MT)
+
+        def load_u(i):
+            nc.sync.dma_start(out=u_raw[i][:].bitcast(I32), in_=u_words[0, :, 2 * K * i : 2 * K * (i + 1)].bitcast(I32))
+
+        def load_v(i, h):
+            c0 = 2 * (N * i + NH * h)
+            nc.sync.dma_start(out=v_sb[i][h][:].bitcast(I32), in_=v_words[0, :, c0 : c0 + 2 * NH].bitcast(I32))
+
+        def load_scale_rows(plane, rows, q):
+            nc.sync.dma_start(out=plane[32 * q : 32 * q + 4, :].bitcast(I32), in_=rows[4 * q : 4 * q + 4, :].bitcast(I32))
 
         def load_x(c):
             nc.sync.dma_start(out=x_sb[c][:], in_=x_view[c])
 
-        def load_w(g):
-            nc.sync.dma_start(out=w_sb[g][:].bitcast(I32), in_=w_words[g].rearrange("p n t -> p (n t)").bitcast(I32))
+        def load_w(h):
+            words = w_words.rearrange("g p n t -> p g (n t)").bitcast(I32)
+            nc.sync.dma_start(out=w_sb[h][:], in_=words[:, :, NH * h : NH * (h + 1)])
 
-        nc.gpsimd.memset(ws_sb[:].rearrange("p g n -> p (g n)").bitcast(I32), 0)
-        nc.gpsimd.dma_start(out=lim_bf[:], in_=lim.rearrange("i (g p t) -> p i g t", g=G, t=4))
+        nc.vector.memset(lim_rows[:].bitcast(I32), 0)
+        nc.vector.memset(us_raw[:].bitcast(I32), 0)
+        nc.vector.memset(vs_sb[:].bitcast(I32), 0)
+        nc.vector.memset(ws_sb[:].rearrange("p g n -> p (g n)").bitcast(I32), 0)
+        nc.gpsimd.dma_start(out=lim_rows[0 : T * G, :], in_=lim.rearrange("i (g c) -> (i g) c", g=G))
         make_identity(nc, ident[:])
-        load_u(0, nc.sync)
-        load_v(0, 0, nc.sync)
+        load_v(0, 0)
+        load_u(0)
         for q in range(4):
-            nc.sync.dma_start(out=us_raw[32 * q : 32 * q + 4, :].bitcast(I32), in_=u_scales[0, 4 * q : 4 * q + 4, :].bitcast(I32))
+            load_scale_rows(us_raw, u_scales[0], q)
         for q in range(4):
-            nc.scalar.dma_start(out=vs_sb[32 * q : 32 * q + 4, :].bitcast(I32), in_=v_scales[0, 4 * q : 4 * q + 4, :].bitcast(I32))
+            load_scale_rows(vs_sb, v_scales[0], q)
+        load_u(1)
         load_x(0)
+        load_v(1, 0)
         load_x(1)
-        load_u(1, nc.sync)
-        load_v(1, 0, nc.sync)
         load_x(2)
         load_x(3)
         for q in range(4):
@@ -110,90 +101,113 @@ def tile_clipped_task_arithmetic_s4_kernel(
                 in_=w_scales[:, 4 * q : 4 * q + 4, :].rearrange("g r n -> r g n").bitcast(I32),
             )
         load_w(0)
+        nc.sync.dma_start(out=lam_sb[:], in_=lam.rearrange("(p m) i -> p (m i)", m=MT))
+        load_v(0, 1)
         load_w(1)
-        nc.sync.dma_start(out=lam_bf[:], in_=lam.rearrange("(p m) i -> p (m i)", m=MT))
-        load_v(0, 1, nc.sync)
-        load_v(1, 1, nc.sync)
-
-        nc.gpsimd.tensor_copy(out=lam_f[:], in_=lam_bf[:])
+        load_v(1, 1)
 
         units = [(h, i, g) for h in range(H) for i in range(T) for g in range(G)]
 
-        def order_u(i, g, eng):
-            eng.tensor_copy(
-                out=u_ord[i][:, g, :, :, :],
-                in_=u_raw[i][:, 1024 * g : 1024 * (g + 1)].rearrange("p (m t b) -> p t m b", t=4, b=2),
+        def order_u(i, g):
+            nc.vector.tensor_copy(
+                out=u_ord[i][g][:].bitcast(U16),
+                in_=u_raw[i][:, 1024 * g : 1024 * (g + 1)].bitcast(U16).rearrange("p (m t) -> p t m", t=4),
             )
-            eng.tensor_copy(
-                out=us_ord[i][:, g, :, :],
+            nc.vector.tensor_copy(
+                out=us_ord[i][g][:],
                 in_=us_raw[:, K * i + 512 * g : K * i + 512 * (g + 1)].rearrange("p (m t) -> p t m", t=4),
             )
+
+        def turn_limits():
+            ps = psum.tile([P, 2, P], F32, name="ps")
+            words = lim_rows[:].bitcast(F32)
+            for u in range(2):
+                nc.tensor.transpose(ps[:, u, :], words[:, u::2], ident[:])
+            nc.scalar.copy(out=lim_hi[:].bitcast(F32), in_=ps[:, :, 0 : T * G].rearrange("p u r -> p r u"))
+            nc.vector.tensor_scalar(out=lim_lo[:], in0=lim_hi[:], scalar1=-1.0, scalar2=None, op0=ALU.mult)
 
         d_sb = {}
         grp = {}
 
-        def task_vectors(j, on_vector=(), ts=range(4)):
+        def clip(j, t, src):
+            h, i, g = units[j]
+            nc.vector.tensor_scalar(
+                out=d_sb[j][:, t, :],
+                in0=src,
+                scalar1=lim_hi[:, i * G + g, t : t + 1],
+                scalar2=lim_lo[:, i * G + g, t : t + 1],
+                op0=ALU.min,
+                op1=ALU.max,
+            )
+
+        d_ps = {}
+
+        def task_vectors(j, ts=range(4)):
             h, i, g = units[j]
             if j not in d_sb:
                 d_sb[j] = work.tile([P, 4, NH], BF16, name="d_sb", align_bytes=64)
             for t in ts:
-                ps = psum_d.tile([P, NH], F32, name="ps_d")
+                d_ps[j, t] = psum.tile([P, NH], F32, name="ps")
                 nc.tensor.matmul_mx(
-                    out=ps[:],
-                    lhsT=u_ord[i][:, g, t, :, :].rearrange("p m b -> p (m b)").bitcast(E2M1),
-                    lhsT_scale=us_ord[i][:, g, t, :],
+                    out=d_ps[j, t][:],
+                    lhsT=u_ord[i][g][:, t, :].bitcast(E2M1),
+                    lhsT_scale=us_ord[i][g][:, t, :],
                     rhs=v_sb[i][h][:].bitcast(E2M1),
                     rhs_scale=vs_sb[:, N * i + NH * h : N * i + NH * (h + 1)],
                     start=True,
                     stop=True,
                 )
-                if t in on_vector:
-                    clip(j, t, ps[:])
-                else:
-                    nc.scalar.copy(out=d_sb[j][:, t, :], in_=ps[:])
 
-        def clip(j, t, src):
-            h, i, g = units[j]
-            c = (i * G + g) * 4 + t
-            eng = nc.gpsimd if (j, t) in GCL else nc.vector
-            eng.tensor_scalar(
-                out=d_sb[j][:, t, :], in0=src, scalar1=lim_hi[:, c : c + 1], scalar2=lim_lo[:, c : c + 1], op0=ALU.min, op1=ALU.max
-            )
+        def copy_out(j, ts=range(4)):
+            for t in ts:
+                nc.scalar.copy(out=d_sb[j][:, t, :], in_=d_ps[j, t][:])
 
-        def clip_rest(j, on_vector):
+        def clip_out(j, ts=range(4)):
+            for t in ts:
+                clip(j, t, d_ps[j, t][:])
+
+        def clip_unit(j):
             for t in range(4):
-                if t not in on_vector:
-                    clip(j, t, d_sb[j][:, t, :])
+                clip(j, t, d_sb[j][:, t, :])
 
-        def interleave(j, cols, scalar_cols):
-            grp[j] = work.tile([P, NH, 4], BF16, name="grp", align_bytes=64)
-            if cols > 0:
-                nc.vector.tensor_copy(
-                    out=grp[j][:, 0:cols, :].rearrange("p (c i) t -> p c t i", i=4), in_=d_sb[j][:, :, 0:cols].rearrange("p t (c i) -> p c t i", i=4)
+        def four_by_four(j, c0, c1):
+            dst = grp[j][:, c0:c1, :].rearrange("p (c i) t -> p c t i", i=4)
+            src = d_sb[j][:, :, c0:c1].rearrange("p t (c i) -> p c t i", i=4)
+            return dst, src
+
+        def interleave_gpsimd(j, cols):
+            grp[j] = keep.tile([P, NH, 4], BF16, name="grp", align_bytes=64)
+            for c0 in range(0, cols, PIECE):
+                nc.gpsimd.tensor_scalar(
+                    out=grp[j][:, c0 : c0 + PIECE, :],
+                    in0=d_sb[j][:, :, c0 : c0 + PIECE].rearrange("p t n -> p n t"),
+                    scalar1=1.0,
+                    scalar2=0.0,
+                    op0=ALU.mult,
+                    op1=ALU.add,
                 )
-            if scalar_cols:
-                nc.scalar.copy(
-                    out=grp[j][:, cols:NH, :].rearrange("p (c i) t -> p c t i", i=4), in_=d_sb[j][:, :, cols:NH].rearrange("p t (c i) -> p c t i", i=4)
-                )
+
+        def interleave_scalar(j, cols):
+            dst, src = four_by_four(j, cols, NH)
+            nc.scalar.copy(out=dst, in_=src)
 
         def quantize(j):
             nc.vector.quantize_mx(out=cq[j][:].bitcast(E4M3), scales=cs[j][:], in_=grp[j][:].rearrange("p n t -> p (n t)"))
 
         xg = {}
 
-        def turn_x(m):
-            c, mm = divmod(m, 2)
-            if mm == 0:
-                xg[c] = work.tile([P, 4, P, 4], BF16, name="xg", align_bytes=64)
-            ps = psum_z.tile([P, G, 2, P], F32, name="ps_z")
-            words = x_sb[c][:, mm, :].bitcast(F32)
-            for g in range(G):
-                for u in range(2):
-                    nc.tensor.transpose(ps[:, g, u, :], words[:, 256 * g + u : 256 * (g + 1) : 2], ident[:])
-            nc.scalar.copy(
-                out=xg[c][:, 2 * mm : 2 * mm + 2, :, :].bitcast(F32),
-                in_=ps[:].rearrange("p g u n -> p g n u"),
-            )
+        def turn_x(c):
+            xg[c] = keep.tile([P, 4, P, 4], BF16, name=f"xg{c}", align_bytes=64)
+            for mm in range(2):
+                ps = psum.tile([P, G, 2, P], F32, name="ps")
+                words = x_sb[c][:, mm, :].bitcast(F32)
+                for g in range(G):
+                    for u in range(2):
+                        nc.tensor.transpose(ps[:, g, u, :], words[:, 256 * g + u : 256 * (g + 1) : 2], ident[:])
+                nc.scalar.copy(
+                    out=xg[c][:, 2 * mm : 2 * mm + 2, :, :].bitcast(F32),
+                    in_=ps[:].rearrange("p g u n -> p g n u"),
+                )
 
         def quantize_x(c):
             nc.vector.quantize_mx(
@@ -202,127 +216,108 @@ def tile_clipped_task_arithmetic_s4_kernel(
                 in_=xg[c][:].rearrange("p a n t -> p (a n t)"),
             )
 
-        def x_times(m, rhs, rhs_scale, cols=slice(0, NH)):
+        def x_pass(ps, m, g, rhs, rhs_scale, cols):
             c, mm = divmod(m, 2)
-            ps = psum_z.tile([P, NH], F32, name="ps_z")
-            for g in range(G):
-                nc.tensor.matmul_mx(
-                    out=ps[:, cols],
-                    lhsT=xq[c][:, 2 * mm + g, :].bitcast(E4M3),
-                    lhsT_scale=xs[c][:, 2 * mm + g, :],
-                    rhs=rhs[g][:, cols].bitcast(E4M3),
-                    rhs_scale=rhs_scale[g][:, cols],
-                    start=(g == 0),
-                    stop=(g == G - 1),
-                )
-            return ps
+            nc.tensor.matmul_mx(
+                out=ps[:, cols],
+                lhsT=xq[c][:, 2 * mm + g, :].bitcast(E4M3),
+                lhsT_scale=xs[c][:, 2 * mm + g, :],
+                rhs=rhs[:, cols].bitcast(E4M3),
+                rhs_scale=rhs_scale[:, cols],
+                start=(g == 0),
+                stop=(g == G - 1),
+            )
 
         def base(h, m):
-            ps = x_times(
-                m,
-                [w_sb[g][:].bitcast(U32)[:, NH * h : NH * (h + 1)] for g in range(G)],
-                [ws_sb[:, g, NH * h : NH * (h + 1)] for g in range(G)],
-            )
+            ps = psum.tile([P, NH], F32, name="ps")
+            for g in range(G):
+                x_pass(ps, m, g, w_sb[h][:, g, :], ws_sb[:, g, NH * h : NH * (h + 1)], slice(0, NH))
             nc.scalar.copy(out=acc[h][m][:], in_=ps[:])
 
-        out_view = out.rearrange("(p m) n -> m p n", m=MT)
+        z_ps = {}
 
-        late = []
+        def task_pass(pair, m, g, cols=slice(0, NH)):
+            if g == 0:
+                z_ps[pair, m] = psum.tile([P, NH], F32, name="ps")
+            x_pass(z_ps[pair, m], m, g, cq[G * pair + g], cs[G * pair + g], cols)
 
-        def task(pair, m, on_scalar=False, cols=slice(0, NH)):
+        def add_task(pair, m, cols=slice(0, NH)):
             h, i = divmod(pair, T)
-            ps = x_times(
-                m,
-                [cq[2 * pair + g] for g in range(G)],
-                [cs[2 * pair + g] for g in range(G)],
-                cols,
+            nc.vector.scalar_tensor_tensor(
+                out=acc[h][m][:, cols],
+                in0=z_ps[pair, m][:, cols],
+                scalar=lam_sb[:, m * T + i : m * T + i + 1],
+                in1=acc[h][m][:, cols],
+                op0=ALU.mult,
+                op1=ALU.add,
             )
-            lam_col = lam_f[:, m * T + i : m * T + i + 1]
-            if on_scalar:
-                part = work.tile([P, NH], F32, name="part", align_bytes=64)
-                nc.scalar.activation(out=part[:], in_=ps[:], func=ACT.Copy, scale=lam_col)
-                nc.gpsimd.tensor_tensor(out=acc[h][m][:], in0=acc[h][m][:], in1=part[:], op=ALU.add)
-            else:
-                nc.vector.scalar_tensor_tensor(out=acc[h][m][:, cols], in0=ps[:, cols], scalar=lam_col, in1=acc[h][m][:, cols], op0=ALU.mult, op1=ALU.add)
             if i == T - 1:
-                late.append((h, m, cols))
-                if not on_scalar:
-                    store(late.pop())
-                    if len(late) > 0 and m - late[0][1] >= 2:
-                        store(late.pop(0))
+                nc.sync.dma_start(out=out_view[m][:, NH * h + cols.start : NH * h + cols.stop], in_=acc[h][m][:, cols])
 
-        def store(hm):
-            h, m, cols = hm
-            nc.sync.dma_start(out=out_view[m][:, NH * h + cols.start : NH * h + cols.stop], in_=acc[h][m][:, cols])
+        def task(pair, m, cols=slice(0, NH)):
+            for g in range(G):
+                task_pass(pair, m, g, cols)
+            add_task(pair, m, cols)
 
-        nc.scalar.activation(out=act_dummy[:], in_=warm[:, 0:1], func=ACT.Copy, scale=1.0)
-        nc.vector.quantize_mx(out=warm_q[:].bitcast(E4M3), scales=warm_s[:], in_=warm[:])
-        ps_warm = psum_d.tile([P, NH], F32, name="ps_d")
-
-        def keep_warm(passes):
-            for r in range(passes):
-                nc.tensor.matmul_mx(
-                    out=ps_warm[:, 0:P], lhsT=warm_q[:].bitcast(E4M3), lhsT_scale=warm_s[:], rhs=warm_q[:].bitcast(E4M3), rhs_scale=warm_s[:], start=True, stop=True
-                )
-
-        keep_warm(WARM)
-        order_u(0, 0, nc.vector)
-        order_u(0, 1, nc.vector)
-        lim_cols = lim_bf[:].rearrange("p i g t -> p (i g t)")
-        nc.vector.tensor_copy(out=lim_hi[:], in_=lim_cols)
-        nc.vector.tensor_scalar(out=lim_lo[:], in0=lim_cols, scalar1=-1.0, scalar2=None, op0=ALU.mult)
-        order_u(1, 0, nc.vector)
-        order_u(1, 1, nc.vector)
-        task_vectors(0, ONV[0])
-        for m in range(0, 4):
-            turn_x(m)
-        task_vectors(1, ONV[1])
-        clip_rest(0, ONV[0])
-        clip_rest(1, ONV[1])
+        order_u(0, 0)
+        order_u(0, 1)
+        turn_limits()
+        task_vectors(0)
+        copy_out(0)
+        order_u(1, 0)
+        order_u(1, 1)
+        task_vectors(1)
+        clip_out(1, (0, 1))
+        clip_unit(0)
+        interleave_gpsimd(0, GP_COLS)
+        clip_out(1, (2, 3))
+        turn_x(0)
+        interleave_scalar(0, GP_COLS)
+        task_vectors(2, (0, 1))
+        clip_out(2, (0, 1))
+        turn_x(1)
         quantize_x(0)
-        interleave(0, VCS[0], VCS[0] < NH)
-        quantize_x(1)
         quantize(0)
-        for m in range(4, 8):
-            turn_x(m)
-        interleave(1, VCS[1], VCS[1] < NH)
-        quantize_x(2)
-        quantize(1)
-        quantize_x(3)
-        task_vectors(2, ONV[2])
-        clip_rest(2, ONV[2])
+        interleave_gpsimd(1, GP_COLS)
+        interleave_scalar(1, GP_COLS)
+        task_vectors(2, (2, 3))
+        clip_out(2, (2, 3))
+        turn_x(2)
         base(0, 0)
-        interleave(2, VCS[2], VCS[2] < NH)
-        for m in range(1, 8):
-            if m == POS:
-                task_vectors(3, ONV[3])
-                quantize(2)
-            base(0, m)
-        ym = 0
-        for k in range(8):
-            pair, first = divmod(k, 2)
-            ms = range(4 * first, 4 * first + 4)
-            j = k + 3
-            if j < 8:
-                clip_rest(j, ONV[j])
-            task(pair, ms[0], (k, 0) in SG)
-            if j + 1 < 8:
-                task_vectors(j + 1, ONV[j + 1], (0, 1))
-            if j < 8:
-                interleave(j, VCS[j], VCS[j] < NH)
-            task(pair, ms[1], (k, 1) in SG)
-            if j + 1 < 8:
-                task_vectors(j + 1, ONV[j + 1], (2, 3))
-            task(pair, ms[2], (k, 2) in SG)
-            if j < 8:
-                quantize(j)
-            for r in range(YS[k]):
-                base(1, ym)
-                ym += 1
-            if k < 7:
-                task(pair, ms[3], (k, 3) in SG)
+        base(0, 1)
+        quantize_x(1)
+        turn_x(3)
+        base(0, 2)
+        base(0, 3)
+        quantize_x(2)
+        last = H * T - 1
+        ahead = ((4, 5), (6, 7), (8, 9), (10,), (11,), (12, 13))
+        for step in range(2 * last):
+            pair, half = divmod(step, 2)
+            share = GP_COLS if step + 3 < UNITS else NH // 2
+            quantize(step + 1)
+            if step == 0:
+                quantize_x(3)
             else:
-                task(pair, ms[3], cols=slice(0, NH // 2))
-                task(pair, ms[3], cols=slice(NH // 2, NH))
-        for hm in late:
-            store(hm)
+                clip_unit(step + 2)
+            interleave_gpsimd(step + 2, share)
+            for b in ahead[step]:
+                base(*divmod(b, MT))
+            if step + 3 < UNITS:
+                task_vectors(step + 3)
+                copy_out(step + 3)
+                interleave_scalar(step + 2, share)
+                for m in range(4 * half, 4 * half + 4):
+                    task(pair, m)
+        interleave_scalar(UNITS - 1, NH // 2)
+        task(last - 1, 4)
+        base(1, 6)
+        task(last - 1, 5)
+        base(1, 7)
+        quantize(UNITS - 1)
+        task(last - 1, 6)
+        task(last - 1, 7)
+        for m in range(MT - 1):
+            task(last, m)
+        task(last, MT - 1, slice(0, NH // 2))
+        task(last, MT - 1, slice(NH // 2, NH))

@@ -14,6 +14,7 @@ U8 = mybir.dt.uint8
 E4M3 = mybir.dt.float8_e4m3fn_x4
 E2M1 = mybir.dt.float4_e2m1fn_x4
 ALU = mybir.AluOpType
+ACT = mybir.ActivationFunctionType
 
 FLOPS = 2 * M * K * N * (1 + T) + 2 * T * R * K * N
 
@@ -45,9 +46,12 @@ def tile_clipped_task_arithmetic_s4_kernel(
         vs_sb = keep.tile([P, T * N], U8, name="vs_sb", align_bytes=64)
         w_sb = [keep.tile([P, G, NH], I32, name=f"w{h}", align_bytes=64) for h in range(H)]
         ws_sb = keep.tile([P, G, N], U8, name="ws_sb", align_bytes=64)
-        x_sb = [keep.tile([P, 2, K], BF16, name=f"x{c}", align_bytes=64) for c in range(MT // 2)]
-        xq = [keep.tile([P, 4, P], U32, name=f"xq{c}", align_bytes=64) for c in range(MT // 2)]
-        xs = [keep.tile([P, 4, P], U8, name=f"xs{c}", align_bytes=64) for c in range(MT // 2)]
+        x_loads = ((0, 2), (2, 4), (4, 6), (6, 8))
+        x_sb = [keep.tile([P, b - a, K], BF16, name=f"x{a}", align_bytes=64) for a, b in x_loads]
+        x_row = [x_sb[c][:, m - a, :] for c, (a, b) in enumerate(x_loads) for m in range(a, b)]
+        xg = [keep.tile([P, G, P, 4], BF16, name=f"xg{m}", align_bytes=64) for m in range(MT)]
+        xq = [keep.tile([P, G, P], U32, name=f"xq{m}", align_bytes=64) for m in range(MT)]
+        xs = [keep.tile([P, G, P], U8, name=f"xs{m}", align_bytes=64) for m in range(MT)]
         cq = [keep.tile([P, NH], U32, name=f"cq{j}", align_bytes=64) for j in range(UNITS)]
         cs = [keep.tile([P, NH], U8, name=f"cs{j}", align_bytes=64) for j in range(UNITS)]
         acc = [[keep.tile([P, NH], F32, name=f"acc{h}_{m}", align_bytes=64) for m in range(MT)] for h in range(H)]
@@ -56,8 +60,9 @@ def tile_clipped_task_arithmetic_s4_kernel(
         lim_hi = keep.tile([P, T * G, 4], BF16, name="lim_hi")
         lim_lo = keep.tile([P, T * G, 4], BF16, name="lim_lo")
         lam_sb = keep.tile([P, MT * T], BF16, name="lam_sb")
+        lam_f = keep.tile([P, MT * T], F32, name="lam_f")
 
-        x_view = x.rearrange("(p c m) k -> c p m k", c=MT // 2, m=2)
+        x_view = x.rearrange("(p m) k -> p m k", m=MT)
         out_view = out.rearrange("(p m) n -> m p n", m=MT)
 
         def load_u(i):
@@ -67,40 +72,40 @@ def tile_clipped_task_arithmetic_s4_kernel(
             c0 = 2 * (N * i + NH * h)
             nc.sync.dma_start(out=v_sb[i][h][:].bitcast(I32), in_=v_words[0, :, c0 : c0 + 2 * NH].bitcast(I32))
 
-        def load_scale_rows(plane, rows, q):
-            nc.sync.dma_start(out=plane[32 * q : 32 * q + 4, :].bitcast(I32), in_=rows[4 * q : 4 * q + 4, :].bitcast(I32))
+        def load_scale_rows(eng, plane, rows, q):
+            eng.dma_start(out=plane[32 * q : 32 * q + 4, :].bitcast(I32), in_=rows[4 * q : 4 * q + 4, :].bitcast(I32))
 
         def load_x(c):
-            nc.sync.dma_start(out=x_sb[c][:], in_=x_view[c])
+            nc.sync.dma_start(out=x_sb[c][:], in_=x_view[:, x_loads[c][0] : x_loads[c][1], :])
 
         def load_w(h):
             words = w_words.rearrange("g p n t -> p g (n t)").bitcast(I32)
             nc.sync.dma_start(out=w_sb[h][:], in_=words[:, :, NH * h : NH * (h + 1)])
 
-        nc.vector.memset(lim_rows[:].bitcast(I32), 0)
+        make_identity(nc, ident[:])
         nc.vector.memset(us_raw[:].bitcast(I32), 0)
         nc.vector.memset(vs_sb[:].bitcast(I32), 0)
+        nc.vector.memset(lim_rows[:].bitcast(I32), 0)
         nc.vector.memset(ws_sb[:].rearrange("p g n -> p (g n)").bitcast(I32), 0)
         nc.gpsimd.dma_start(out=lim_rows[0 : T * G, :], in_=lim.rearrange("i (g c) -> (i g) c", g=G))
-        make_identity(nc, ident[:])
-        load_v(0, 0)
-        load_u(0)
-        for q in range(4):
-            load_scale_rows(us_raw, u_scales[0], q)
-        for q in range(4):
-            load_scale_rows(vs_sb, v_scales[0], q)
-        load_u(1)
         load_x(0)
-        load_v(1, 0)
+        load_u(0)
+        load_v(0, 0)
+        for q in range(4):
+            load_scale_rows(nc.sync, us_raw, u_scales[0], q)
         load_x(1)
+        for q in range(4):
+            load_scale_rows(nc.sync, vs_sb, v_scales[0], q)
+        load_u(1)
+        load_v(1, 0)
         load_x(2)
-        load_x(3)
+        load_w(0)
         for q in range(4):
             nc.sync.dma_start(
                 out=ws_sb[32 * q : 32 * q + 4, :, :].bitcast(I32),
                 in_=w_scales[:, 4 * q : 4 * q + 4, :].rearrange("g r n -> r g n").bitcast(I32),
             )
-        load_w(0)
+        load_x(3)
         nc.sync.dma_start(out=lam_sb[:], in_=lam.rearrange("(p m) i -> p (m i)", m=MT))
         load_v(0, 1)
         load_w(1)
@@ -118,12 +123,14 @@ def tile_clipped_task_arithmetic_s4_kernel(
                 in_=us_raw[:, K * i + 512 * g : K * i + 512 * (g + 1)].rearrange("p (m t) -> p t m", t=4),
             )
 
-        def turn_limits():
+        def turn_limits_mm():
             ps = psum.tile([P, 2, P], F32, name="ps")
             words = lim_rows[:].bitcast(F32)
             for u in range(2):
                 nc.tensor.transpose(ps[:, u, :], words[:, u::2], ident[:])
             nc.scalar.copy(out=lim_hi[:].bitcast(F32), in_=ps[:, :, 0 : T * G].rearrange("p u r -> p r u"))
+
+        def turn_limits_neg():
             nc.vector.tensor_scalar(out=lim_lo[:], in0=lim_hi[:], scalar1=-1.0, scalar2=None, op0=ALU.mult)
 
         d_sb = {}
@@ -166,8 +173,8 @@ def tile_clipped_task_arithmetic_s4_kernel(
             for t in ts:
                 clip(j, t, d_ps[j, t][:])
 
-        def clip_unit(j):
-            for t in range(4):
+        def clip_unit(j, ts=range(4)):
+            for t in ts:
                 clip(j, t, d_sb[j][:, t, :])
 
         def four_by_four(j, c0, c1):
@@ -191,37 +198,33 @@ def tile_clipped_task_arithmetic_s4_kernel(
             dst, src = four_by_four(j, cols, NH)
             nc.scalar.copy(out=dst, in_=src)
 
+        def interleave_vector(j, cols):
+            dst, src = four_by_four(j, cols, NH)
+            nc.vector.tensor_copy(out=dst, in_=src)
+
         def quantize(j):
             nc.vector.quantize_mx(out=cq[j][:].bitcast(E4M3), scales=cs[j][:], in_=grp[j][:].rearrange("p n t -> p (n t)"))
 
-        xg = {}
+        def turn_x(m):
+            ps = psum.tile([P, G, 2, P], F32, name="ps")
+            words = x_row[m].bitcast(F32)
+            for g in range(G):
+                for u in range(2):
+                    nc.tensor.transpose(ps[:, g, u, :], words[:, 256 * g + u : 256 * (g + 1) : 2], ident[:])
+            nc.scalar.copy(out=xg[m][:].bitcast(F32), in_=ps[:].rearrange("p g u n -> p g n u"))
 
-        def turn_x(c):
-            xg[c] = keep.tile([P, 4, P, 4], BF16, name=f"xg{c}", align_bytes=64)
-            for mm in range(2):
-                ps = psum.tile([P, G, 2, P], F32, name="ps")
-                words = x_sb[c][:, mm, :].bitcast(F32)
-                for g in range(G):
-                    for u in range(2):
-                        nc.tensor.transpose(ps[:, g, u, :], words[:, 256 * g + u : 256 * (g + 1) : 2], ident[:])
-                nc.scalar.copy(
-                    out=xg[c][:, 2 * mm : 2 * mm + 2, :, :].bitcast(F32),
-                    in_=ps[:].rearrange("p g u n -> p g n u"),
-                )
-
-        def quantize_x(c):
+        def quantize_x(m):
             nc.vector.quantize_mx(
-                out=xq[c][:].rearrange("p a n -> p (a n)").bitcast(E4M3),
-                scales=xs[c][:].rearrange("p a n -> p (a n)"),
-                in_=xg[c][:].rearrange("p a n t -> p (a n t)"),
+                out=xq[m][:].rearrange("p g n -> p (g n)").bitcast(E4M3),
+                scales=xs[m][:].rearrange("p g n -> p (g n)"),
+                in_=xg[m][:].rearrange("p g n t -> p (g n t)"),
             )
 
         def x_pass(ps, m, g, rhs, rhs_scale, cols):
-            c, mm = divmod(m, 2)
             nc.tensor.matmul_mx(
                 out=ps[:, cols],
-                lhsT=xq[c][:, 2 * mm + g, :].bitcast(E4M3),
-                lhsT_scale=xs[c][:, 2 * mm + g, :],
+                lhsT=xq[m][:, g, :].bitcast(E4M3),
+                lhsT_scale=xs[m][:, g, :],
                 rhs=rhs[:, cols].bitcast(E4M3),
                 rhs_scale=rhs_scale[:, cols],
                 start=(g == 0),
@@ -254,69 +257,81 @@ def tile_clipped_task_arithmetic_s4_kernel(
             if i == T - 1:
                 nc.sync.dma_start(out=out_view[m][:, NH * h + cols.start : NH * h + cols.stop], in_=acc[h][m][:, cols])
 
+        def task_beside(pair, m):
+            h, i = divmod(pair, T)
+            for g in range(G):
+                task_pass(pair, m, g)
+            part = work.tile([P, NH], F32, name="part", align_bytes=64)
+            nc.scalar.activation(out=part[:], in_=z_ps[pair, m][:], func=ACT.Copy, scale=lam_f[:, m * T + i : m * T + i + 1])
+            nc.gpsimd.tensor_tensor(out=acc[h][m][:], in0=acc[h][m][:], in1=part[:], op=ALU.add)
+
         def task(pair, m, cols=slice(0, NH)):
             for g in range(G):
                 task_pass(pair, m, g, cols)
             add_task(pair, m, cols)
 
-        order_u(0, 0)
-        order_u(0, 1)
-        turn_limits()
-        task_vectors(0)
-        copy_out(0)
-        order_u(1, 0)
-        order_u(1, 1)
-        task_vectors(1)
-        clip_out(1, (0, 1))
-        clip_unit(0)
-        interleave_gpsimd(0, GP_COLS)
-        clip_out(1, (2, 3))
         turn_x(0)
-        interleave_scalar(0, GP_COLS)
-        task_vectors(2, (0, 1))
-        clip_out(2, (0, 1))
         turn_x(1)
+        order_u(0, 0)
         quantize_x(0)
-        quantize(0)
-        interleave_gpsimd(1, GP_COLS)
-        interleave_scalar(1, GP_COLS)
-        task_vectors(2, (2, 3))
-        clip_out(2, (2, 3))
-        turn_x(2)
-        base(0, 0)
-        base(0, 1)
         quantize_x(1)
+        order_u(0, 1)
+        turn_limits_mm()
+        turn_limits_neg()
+        turn_x(2)
         turn_x(3)
-        base(0, 2)
-        base(0, 3)
+        task_vectors(0)
+        order_u(1, 0)
+        clip_out(0, (0, 1))
+        copy_out(0, (2, 3))
+        order_u(1, 1)
+        clip_unit(0, (2, 3))
+        interleave_gpsimd(0, GP_COLS)
+        task_vectors(1)
+        clip_out(1)
+        interleave_scalar(0, GP_COLS)
+        turn_x(4)
+        turn_x(5)
         quantize_x(2)
+        quantize(0)
+        quantize_x(3)
+        interleave_gpsimd(1, GP_COLS)
+        task_vectors(2)
+        copy_out(2, (0, 1))
+        clip_out(2, (2, 3))
+        for m in range(4):
+            base(0, m)
+        interleave_scalar(1, GP_COLS)
+        turn_x(6)
+        turn_x(7)
+        clip_unit(2, (0, 1))
+        quantize(1)
+        interleave_gpsimd(2, GP_COLS)
+        quantize_x(4)
+        quantize_x(5)
         last = H * T - 1
-        ahead = ((4, 5), (6, 7), (8, 9), (10,), (11,), (12, 13))
         for step in range(2 * last):
             pair, half = divmod(step, 2)
-            share = GP_COLS if step + 3 < UNITS else NH // 2
-            quantize(step + 1)
-            if step == 0:
-                quantize_x(3)
-            else:
-                clip_unit(step + 2)
-            interleave_gpsimd(step + 2, share)
-            for b in ahead[step]:
-                base(*divmod(b, MT))
+            tiles = range(4 * half, 4 * half + 4)
+            interleave_scalar(step + 2, GP_COLS)
             if step + 3 < UNITS:
                 task_vectors(step + 3)
                 copy_out(step + 3)
-                interleave_scalar(step + 2, share)
-                for m in range(4 * half, 4 * half + 4):
-                    task(pair, m)
-        interleave_scalar(UNITS - 1, NH // 2)
-        task(last - 1, 4)
-        base(1, 6)
-        task(last - 1, 5)
-        base(1, 7)
-        quantize(UNITS - 1)
-        task(last - 1, 6)
-        task(last - 1, 7)
+            for n in range(2):
+                task(pair, tiles[n])
+                base(*divmod(4 + 2 * step + n, MT))
+            quantize(step + 2)
+            if step == 0:
+                quantize_x(6)
+                quantize_x(7)
+                nc.vector.tensor_copy(out=lam_f[:], in_=lam_sb[:])
+            if step + 3 < UNITS:
+                clip_unit(step + 3)
+                interleave_gpsimd(step + 3, GP_COLS)
+                task(pair, tiles[2])
+                task(pair, tiles[3])
+        task_beside(last - 1, MT - 2)
+        task_beside(last - 1, MT - 1)
         for m in range(MT - 1):
             task(last, m)
         task(last, MT - 1, slice(0, NH // 2))

@@ -24,8 +24,8 @@ MT = M // P
 G = K // 512
 H = N // NH
 UNITS = H * T * G
-PIECE = 128
-GP_COLS = 384
+GP_COLS = 256
+SC_COLS = 128
 
 
 def tile_clipped_task_arithmetic_s4_kernel(
@@ -82,30 +82,30 @@ def tile_clipped_task_arithmetic_s4_kernel(
             words = w_words.rearrange("g p n t -> p g (n t)").bitcast(I32)
             nc.sync.dma_start(out=w_sb[h][:], in_=words[:, :, NH * h : NH * (h + 1)])
 
-        make_identity(nc, ident[:])
+        nc.vector.memset(lim_rows[:].bitcast(I32), 0)
         nc.vector.memset(us_raw[:].bitcast(I32), 0)
         nc.vector.memset(vs_sb[:].bitcast(I32), 0)
-        nc.vector.memset(lim_rows[:].bitcast(I32), 0)
         nc.vector.memset(ws_sb[:].rearrange("p g n -> p (g n)").bitcast(I32), 0)
         nc.gpsimd.dma_start(out=lim_rows[0 : T * G, :], in_=lim.rearrange("i (g c) -> (i g) c", g=G))
-        load_x(0)
-        load_u(0)
+        make_identity(nc, ident[:])
         load_v(0, 0)
+        load_u(0)
         for q in range(4):
             load_scale_rows(nc.sync, us_raw, u_scales[0], q)
-        load_x(1)
         for q in range(4):
             load_scale_rows(nc.sync, vs_sb, v_scales[0], q)
         load_u(1)
+        load_x(0)
         load_v(1, 0)
+        load_x(1)
         load_x(2)
-        load_w(0)
+        load_x(3)
         for q in range(4):
             nc.sync.dma_start(
                 out=ws_sb[32 * q : 32 * q + 4, :, :].bitcast(I32),
                 in_=w_scales[:, 4 * q : 4 * q + 4, :].rearrange("g r n -> r g n").bitcast(I32),
             )
-        load_x(3)
+        load_w(0)
         nc.sync.dma_start(out=lam_sb[:], in_=lam.rearrange("(p m) i -> p (m i)", m=MT))
         load_v(0, 1)
         load_w(1)
@@ -182,25 +182,24 @@ def tile_clipped_task_arithmetic_s4_kernel(
             src = d_sb[j][:, :, c0:c1].rearrange("p t (c i) -> p c t i", i=4)
             return dst, src
 
-        def interleave_gpsimd(j, cols):
+        def interleave_gpsimd(j):
             grp[j] = keep.tile([P, NH, 4], BF16, name="grp", align_bytes=64)
-            for c0 in range(0, cols, PIECE):
-                nc.gpsimd.tensor_scalar(
-                    out=grp[j][:, c0 : c0 + PIECE, :],
-                    in0=d_sb[j][:, :, c0 : c0 + PIECE].rearrange("p t n -> p n t"),
-                    scalar1=1.0,
-                    scalar2=0.0,
-                    op0=ALU.mult,
-                    op1=ALU.add,
-                )
+            nc.gpsimd.tensor_scalar(
+                out=grp[j][:, 0:GP_COLS, :],
+                in0=d_sb[j][:, :, 0:GP_COLS].rearrange("p t n -> p n t"),
+                scalar1=1.0,
+                scalar2=0.0,
+                op0=ALU.mult,
+                op1=ALU.add,
+            )
 
-        def interleave_scalar(j, cols):
-            dst, src = four_by_four(j, cols, NH)
-            nc.scalar.copy(out=dst, in_=src)
-
-        def interleave_vector(j, cols):
-            dst, src = four_by_four(j, cols, NH)
+        def interleave_vector(j):
+            dst, src = four_by_four(j, GP_COLS, NH - SC_COLS)
             nc.vector.tensor_copy(out=dst, in_=src)
+
+        def interleave_scalar(j, first=NH - SC_COLS):
+            dst, src = four_by_four(j, first, NH)
+            nc.scalar.copy(out=dst, in_=src)
 
         def quantize(j):
             nc.vector.quantize_mx(out=cq[j][:].bitcast(E4M3), scales=cs[j][:], in_=grp[j][:].rearrange("p n t -> p (n t)"))
@@ -270,66 +269,75 @@ def tile_clipped_task_arithmetic_s4_kernel(
                 task_pass(pair, m, g, cols)
             add_task(pair, m, cols)
 
-        turn_x(0)
-        turn_x(1)
         order_u(0, 0)
-        quantize_x(0)
-        quantize_x(1)
         order_u(0, 1)
         turn_limits_mm()
+        task_vectors(0)
+        copy_out(0)
         turn_limits_neg()
+        order_u(1, 0)
+        order_u(1, 1)
+        task_vectors(1)
+        clip_out(1, (0, 1))
+        clip_unit(0)
+        interleave_gpsimd(0)
+        clip_out(1, (2, 3))
+        turn_x(0)
+        turn_x(1)
+        interleave_scalar(0)
+        task_vectors(2, (0, 1))
+        clip_out(2, (0, 1))
         turn_x(2)
         turn_x(3)
-        task_vectors(0)
-        order_u(1, 0)
-        clip_out(0, (0, 1))
-        copy_out(0, (2, 3))
-        order_u(1, 1)
-        clip_unit(0, (2, 3))
-        interleave_gpsimd(0, GP_COLS)
-        task_vectors(1)
-        clip_out(1)
-        interleave_scalar(0, GP_COLS)
+        interleave_vector(0)
+        quantize_x(0)
+        quantize_x(1)
+        quantize(0)
+        interleave_gpsimd(1)
+        interleave_scalar(1)
+        task_vectors(2, (2, 3))
+        clip_out(2, (2, 3))
         turn_x(4)
         turn_x(5)
+        base(0, 0)
+        base(0, 1)
+        interleave_vector(1)
         quantize_x(2)
-        quantize(0)
         quantize_x(3)
-        interleave_gpsimd(1, GP_COLS)
-        task_vectors(2)
-        copy_out(2, (0, 1))
-        clip_out(2, (2, 3))
-        for m in range(4):
-            base(0, m)
-        interleave_scalar(1, GP_COLS)
         turn_x(6)
         turn_x(7)
-        clip_unit(2, (0, 1))
-        quantize(1)
-        interleave_gpsimd(2, GP_COLS)
+        base(0, 2)
+        base(0, 3)
         quantize_x(4)
         quantize_x(5)
+        quantize(1)
+        interleave_gpsimd(2)
         last = H * T - 1
-        for step in range(2 * last):
+        for step in range(UNITS - 3):
             pair, half = divmod(step, 2)
             tiles = range(4 * half, 4 * half + 4)
-            interleave_scalar(step + 2, GP_COLS)
-            if step + 3 < UNITS:
-                task_vectors(step + 3)
-                copy_out(step + 3)
+            task_vectors(step + 3)
+            copy_out(step + 3)
+            interleave_scalar(step + 2)
             for n in range(2):
                 task(pair, tiles[n])
                 base(*divmod(4 + 2 * step + n, MT))
-            quantize(step + 2)
+            interleave_vector(step + 2)
             if step == 0:
                 quantize_x(6)
                 quantize_x(7)
                 nc.vector.tensor_copy(out=lam_f[:], in_=lam_sb[:])
-            if step + 3 < UNITS:
-                clip_unit(step + 3)
-                interleave_gpsimd(step + 3, GP_COLS)
-                task(pair, tiles[2])
-                task(pair, tiles[3])
+            clip_unit(step + 3)
+            quantize(step + 2)
+            interleave_gpsimd(step + 3)
+            task(pair, tiles[2])
+            task(pair, tiles[3])
+        interleave_scalar(UNITS - 1, GP_COLS)
+        task(last - 1, MT - 4)
+        base(1, MT - 2)
+        quantize(UNITS - 1)
+        task(last - 1, MT - 3)
+        base(1, MT - 1)
         task_beside(last - 1, MT - 2)
         task_beside(last - 1, MT - 1)
         for m in range(MT - 1):

@@ -26,6 +26,7 @@ H = N // NH
 UNITS = H * T * G
 GP_COLS = 256
 SC_COLS = 128
+WARM_N = 256
 
 
 def tile_clipped_task_arithmetic_s4_kernel(
@@ -55,6 +56,8 @@ def tile_clipped_task_arithmetic_s4_kernel(
         cq = [keep.tile([P, NH], U32, name=f"cq{j}", align_bytes=64) for j in range(UNITS)]
         cs = [keep.tile([P, NH], U8, name=f"cs{j}", align_bytes=64) for j in range(UNITS)]
         acc = [[keep.tile([P, NH], F32, name=f"acc{h}_{m}", align_bytes=64) for m in range(MT)] for h in range(H)]
+        warm_q = keep.tile([P, WARM_N], U32, name="warm_q", align_bytes=64)
+        warm_s = keep.tile([P, WARM_N], U8, name="warm_s", align_bytes=64)
         ident = keep.tile([P, P], F32, name="ident")
         lim_rows = keep.tile([P, 512], BF16, name="lim_rows")
         lim_hi = keep.tile([P, T * G, 4], BF16, name="lim_hi")
@@ -85,9 +88,11 @@ def tile_clipped_task_arithmetic_s4_kernel(
         nc.vector.memset(lim_rows[:].bitcast(I32), 0)
         nc.vector.memset(us_raw[:].bitcast(I32), 0)
         nc.vector.memset(vs_sb[:].bitcast(I32), 0)
-        nc.vector.memset(ws_sb[:].rearrange("p g n -> p (g n)").bitcast(I32), 0)
+        ws_flat = ws_sb[:].rearrange("p g n -> p (g n)")
+        nc.vector.memset(ws_flat.bitcast(I32), 0)
         nc.gpsimd.dma_start(out=lim_rows[0 : T * G, :], in_=lim.rearrange("i (g c) -> (i g) c", g=G))
         make_identity(nc, ident[:])
+        nc.vector.quantize_mx(out=warm_q[:].bitcast(E4M3), scales=warm_s[:], in_=ws_flat.bitcast(BF16))
         load_v(0, 0)
         load_u(0)
         for q in range(4):
@@ -122,6 +127,19 @@ def tile_clipped_task_arithmetic_s4_kernel(
                 out=us_ord[i][g][:],
                 in_=us_raw[:, K * i + 512 * g : K * i + 512 * (g + 1)].rearrange("p (m t) -> p t m", t=4),
             )
+
+        def warm_up(passes):
+            ps = psum.tile([P, NH], F32, name="ps")
+            for r in range(passes):
+                nc.tensor.matmul_mx(
+                    out=ps[:, 0:WARM_N],
+                    lhsT=warm_q[:, 0:P].bitcast(E4M3),
+                    lhsT_scale=warm_s[:, 0:P],
+                    rhs=warm_q[:].bitcast(E4M3),
+                    rhs_scale=warm_s[:],
+                    start=True,
+                    stop=True,
+                )
 
         def turn_limits_mm():
             ps = psum.tile([P, 2, P], F32, name="ps")
@@ -269,6 +287,7 @@ def tile_clipped_task_arithmetic_s4_kernel(
                 task_pass(pair, m, g, cols)
             add_task(pair, m, cols)
 
+        warm_up(10)
         order_u(0, 0)
         order_u(0, 1)
         turn_limits_mm()

@@ -24,8 +24,7 @@ MT = M // P
 G = K // 512
 H = N // NH
 UNITS = H * T * G
-GP_COLS = 256
-SC_COLS = 128
+GP_COLS = 384
 WARM_N = 256
 
 
@@ -200,22 +199,18 @@ def tile_clipped_task_arithmetic_s4_kernel(
             src = d_sb[j][:, :, c0:c1].rearrange("p t (c i) -> p c t i", i=4)
             return dst, src
 
-        def interleave_gpsimd(j):
+        def interleave_gpsimd(j, cols=GP_COLS):
             grp[j] = keep.tile([P, NH, 4], BF16, name="grp", align_bytes=64)
             nc.gpsimd.tensor_scalar(
-                out=grp[j][:, 0:GP_COLS, :],
-                in0=d_sb[j][:, :, 0:GP_COLS].rearrange("p t n -> p n t"),
+                out=grp[j][:, 0:cols, :],
+                in0=d_sb[j][:, :, 0:cols].rearrange("p t n -> p n t"),
                 scalar1=1.0,
                 scalar2=0.0,
                 op0=ALU.mult,
                 op1=ALU.add,
             )
 
-        def interleave_vector(j):
-            dst, src = four_by_four(j, GP_COLS, NH - SC_COLS)
-            nc.vector.tensor_copy(out=dst, in_=src)
-
-        def interleave_scalar(j, first=NH - SC_COLS):
+        def interleave_scalar(j, first=GP_COLS):
             dst, src = four_by_four(j, first, NH)
             nc.scalar.copy(out=dst, in_=src)
 
@@ -308,7 +303,6 @@ def tile_clipped_task_arithmetic_s4_kernel(
         clip_out(2, (0, 1))
         turn_x(2)
         turn_x(3)
-        interleave_vector(0)
         quantize_x(0)
         quantize_x(1)
         quantize(0)
@@ -320,7 +314,6 @@ def tile_clipped_task_arithmetic_s4_kernel(
         turn_x(5)
         base(0, 0)
         base(0, 1)
-        interleave_vector(1)
         quantize_x(2)
         quantize_x(3)
         turn_x(6)
@@ -341,17 +334,16 @@ def tile_clipped_task_arithmetic_s4_kernel(
             for n in range(2):
                 task(pair, tiles[n])
                 base(*divmod(4 + 2 * step + n, MT))
-            interleave_vector(step + 2)
             if step == 0:
                 quantize_x(6)
                 quantize_x(7)
                 nc.vector.tensor_copy(out=lam_f[:], in_=lam_sb[:])
             clip_unit(step + 3)
             quantize(step + 2)
-            interleave_gpsimd(step + 3)
+            interleave_gpsimd(step + 3, GP_COLS if step + 4 < UNITS else NH // 2)
             task(pair, tiles[2])
             task(pair, tiles[3])
-        interleave_scalar(UNITS - 1, GP_COLS)
+        interleave_scalar(UNITS - 1, NH // 2)
         task(last - 1, MT - 4)
         base(1, MT - 2)
         quantize(UNITS - 1)

@@ -305,24 +305,22 @@ def tile_clipped_task_arithmetic_s4_kernel(
         turn_x(3)
         quantize_x(0)
         quantize_x(1)
+        quantize_x(2)
+        quantize_x(3)
         quantize(0)
         interleave_gpsimd(1)
-        interleave_scalar(1)
         task_vectors(2, (2, 3))
         clip_out(2, (2, 3))
         turn_x(4)
         turn_x(5)
-        base(0, 0)
-        base(0, 1)
-        quantize_x(2)
-        quantize_x(3)
+        interleave_scalar(1)
         turn_x(6)
         turn_x(7)
-        base(0, 2)
-        base(0, 3)
+        for m in range(4):
+            base(0, m)
         quantize_x(4)
-        quantize_x(5)
         quantize(1)
+        quantize_x(5)
         interleave_gpsimd(2)
         last = H * T - 1
         for step in range(UNITS - 3):

@@ -118,10 +118,16 @@ def tile_clipped_task_arithmetic_s4_kernel(
         units = [(h, i, g) for h in range(H) for i in range(T) for g in range(G)]
 
         def order_u(i, g):
+            order_u_codes(i, g)
+            order_u_scales(i, g)
+
+        def order_u_codes(i, g):
             nc.vector.tensor_copy(
                 out=u_ord[i][g][:].bitcast(U16),
                 in_=u_raw[i][:, 1024 * g : 1024 * (g + 1)].bitcast(U16).rearrange("p (m t) -> p t m", t=4),
             )
+
+        def order_u_scales(i, g):
             nc.vector.tensor_copy(
                 out=us_ord[i][g][:],
                 in_=us_raw[:, K * i + 512 * g : K * i + 512 * (g + 1)].rearrange("p (m t) -> p t m", t=4),
@@ -285,12 +291,14 @@ def tile_clipped_task_arithmetic_s4_kernel(
         warm_up(10)
         order_u(0, 0)
         order_u(0, 1)
+        for g in range(G):
+            order_u_scales(1, g)
         turn_limits_mm()
         task_vectors(0)
         copy_out(0)
         turn_limits_neg()
-        order_u(1, 0)
-        order_u(1, 1)
+        for g in range(G):
+            order_u_codes(1, g)
         task_vectors(1)
         clip_out(1, (0, 1))
         clip_unit(0)
@@ -310,37 +318,43 @@ def tile_clipped_task_arithmetic_s4_kernel(
         quantize(0)
         interleave_gpsimd(1)
         task_vectors(2, (2, 3))
-        clip_out(2, (2, 3))
+        copy_out(2, (2, 3))
         turn_x(4)
         turn_x(5)
         interleave_scalar(1)
         turn_x(6)
         turn_x(7)
+        task_vectors(3)
+        clip_out(3)
+        quantize(1)
+        quantize_x(4)
+        quantize_x(5)
+        clip_unit(2, (2, 3))
+        interleave_gpsimd(2)
         for m in range(4):
             base(0, m)
-        quantize_x(4)
-        quantize(1)
-        quantize_x(5)
-        interleave_gpsimd(2)
         last = H * T - 1
         for step in range(UNITS - 3):
             pair, half = divmod(step, 2)
             tiles = range(4 * half, 4 * half + 4)
-            task_vectors(step + 3)
-            copy_out(step + 3)
+            if step > 0:
+                task_vectors(step + 3)
+                copy_out(step + 3)
             interleave_scalar(step + 2)
-            for n in range(2):
+            before = 2 if step < 4 else 1
+            for n in range(4):
+                if n == before:
+                    if step == 0:
+                        quantize_x(6)
+                        quantize_x(7)
+                        nc.vector.tensor_copy(out=lam_f[:], in_=lam_sb[:])
+                    else:
+                        clip_unit(step + 3)
+                    quantize(step + 2)
+                    interleave_gpsimd(step + 3, GP_COLS if step + 4 < UNITS else NH // 2)
                 task(pair, tiles[n])
-                base(*divmod(4 + 2 * step + n, MT))
-            if step == 0:
-                quantize_x(6)
-                quantize_x(7)
-                nc.vector.tensor_copy(out=lam_f[:], in_=lam_sb[:])
-            clip_unit(step + 3)
-            quantize(step + 2)
-            interleave_gpsimd(step + 3, GP_COLS if step + 4 < UNITS else NH // 2)
-            task(pair, tiles[2])
-            task(pair, tiles[3])
+                if n < 2:
+                    base(*divmod(4 + 2 * step + n, MT))
         interleave_scalar(UNITS - 1, NH // 2)
         task(last - 1, MT - 4)
         base(1, MT - 2)
@@ -348,8 +362,8 @@ def tile_clipped_task_arithmetic_s4_kernel(
         task(last - 1, MT - 3)
         base(1, MT - 1)
         task_beside(last - 1, MT - 2)
-        task_beside(last - 1, MT - 1)
         for m in range(MT - 1):
             task(last, m)
-        task(last, MT - 1, slice(0, NH // 2))
-        task(last, MT - 1, slice(NH // 2, NH))
+        for pair in (last - 1, last):
+            task(pair, MT - 1, slice(0, NH // 2))
+            task(pair, MT - 1, slice(NH // 2, NH))

@@ -34,7 +34,7 @@ def tile_clipped_task_arithmetic_s4_kernel(
     nc = tc.nc
     with ExitStack() as ctx:
         keep = ctx.enter_context(tc.tile_pool(name="keep", bufs=1))
-        work = ctx.enter_context(tc.tile_pool(name="work", bufs=3))
+        work = ctx.enter_context(tc.tile_pool(name="work", bufs=4))
         psum = ctx.enter_context(tc.psum_pool(name="psum", bufs=8))
         ctx.enter_context(tc.manual_schedule())
 
@@ -45,7 +45,7 @@ def tile_clipped_task_arithmetic_s4_kernel(
         v_sb = [[keep.tile([P, 2 * NH], U8, name=f"v{i}_{h}", align_bytes=64) for h in range(H)] for i in range(T)]
         vs_sb = keep.tile([P, T * N], U8, name="vs_sb", align_bytes=64)
         w_sb = [keep.tile([P, G, NH], I32, name=f"w{h}", align_bytes=64) for h in range(H)]
-        ws_sb = keep.tile([P, G, N], U8, name="ws_sb", align_bytes=64)
+        ws_sb = keep.tile([P, H, G, NH], U8, name="ws_sb", align_bytes=64)
         x_loads = ((0, 2), (2, 4), (4, 6), (6, 8))
         x_sb = [keep.tile([P, b - a, K], BF16, name=f"x{a}", align_bytes=64) for a, b in x_loads]
         x_row = [x_sb[c][:, m - a, :] for c, (a, b) in enumerate(x_loads) for m in range(a, b)]
@@ -74,8 +74,11 @@ def tile_clipped_task_arithmetic_s4_kernel(
             c0 = 2 * (N * i + NH * h)
             nc.sync.dma_start(out=v_sb[i][h][:].bitcast(I32), in_=v_words[0, :, c0 : c0 + 2 * NH].bitcast(I32))
 
-        def load_scale_rows(eng, plane, rows, q):
-            eng.dma_start(out=plane[32 * q : 32 * q + 4, :].bitcast(I32), in_=rows[4 * q : 4 * q + 4, :].bitcast(I32))
+        def load_scale_rows(plane, rows):
+            for q in range(4):
+                nc.sync.dma_start(out=plane[32 * q : 32 * q + 4].bitcast(I32), in_=rows[4 * q : 4 * q + 4].bitcast(I32))
+
+        ws_rows = w_scales.rearrange("g r (h n) -> r h g n", h=H)
 
         def load_x(c):
             nc.sync.dma_start(out=x_sb[c][:], in_=x_view[:, x_loads[c][0] : x_loads[c][1], :])
@@ -87,32 +90,27 @@ def tile_clipped_task_arithmetic_s4_kernel(
         nc.vector.memset(lim_rows[:].bitcast(I32), 0)
         nc.vector.memset(us_raw[:].bitcast(I32), 0)
         nc.vector.memset(vs_sb[:].bitcast(I32), 0)
-        ws_flat = ws_sb[:].rearrange("p g n -> p (g n)")
+        ws_flat = ws_sb[:].rearrange("p h g n -> p (h g n)")
         nc.vector.memset(ws_flat.bitcast(I32), 0)
         nc.gpsimd.dma_start(out=lim_rows[0 : T * G, :], in_=lim.rearrange("i (g c) -> (i g) c", g=G))
         make_identity(nc, ident[:])
         nc.vector.quantize_mx(out=warm_q[:].bitcast(E4M3), scales=warm_s[:], in_=ws_flat.bitcast(BF16))
         load_v(0, 0)
         load_u(0)
-        for q in range(4):
-            load_scale_rows(nc.sync, us_raw, u_scales[0], q)
-        for q in range(4):
-            load_scale_rows(nc.sync, vs_sb, v_scales[0], q)
+        load_scale_rows(us_raw, u_scales[0])
+        load_scale_rows(vs_sb, v_scales[0])
         load_u(1)
-        load_x(0)
         load_v(1, 0)
+        load_x(0)
         load_x(1)
         load_x(2)
-        load_x(3)
-        for q in range(4):
-            nc.sync.dma_start(
-                out=ws_sb[32 * q : 32 * q + 4, :, :].bitcast(I32),
-                in_=w_scales[:, 4 * q : 4 * q + 4, :].rearrange("g r n -> r g n").bitcast(I32),
-            )
+        load_scale_rows(ws_sb[:, 0], ws_rows[:, 0])
         load_w(0)
+        load_x(3)
         nc.sync.dma_start(out=lam_sb[:], in_=lam.rearrange("(p m) i -> p (m i)", m=MT))
         load_v(0, 1)
         load_w(1)
+        load_scale_rows(ws_sb[:, 1], ws_rows[:, 1])
         load_v(1, 1)
 
         units = [(h, i, g) for h in range(H) for i in range(T) for g in range(G)]
@@ -252,7 +250,7 @@ def tile_clipped_task_arithmetic_s4_kernel(
         def base(h, m):
             ps = psum.tile([P, NH], F32, name="ps")
             for g in range(G):
-                x_pass(ps, m, g, w_sb[h][:, g, :], ws_sb[:, g, NH * h : NH * (h + 1)], slice(0, NH))
+                x_pass(ps, m, g, w_sb[h][:, g, :], ws_sb[:, h, g, :], slice(0, NH))
             nc.scalar.copy(out=acc[h][m][:], in_=ps[:])
 
         z_ps = {}
@@ -288,48 +286,44 @@ def tile_clipped_task_arithmetic_s4_kernel(
                 task_pass(pair, m, g, cols)
             add_task(pair, m, cols)
 
-        warm_up(10)
+        warm_up(7)
         order_u(0, 0)
         order_u(0, 1)
         for g in range(G):
             order_u_scales(1, g)
         turn_limits_mm()
         task_vectors(0)
-        copy_out(0)
+        copy_out(0, (0, 1))
         turn_limits_neg()
+        clip_out(0, (2,))
         for g in range(G):
             order_u_codes(1, g)
-        task_vectors(1)
-        clip_out(1, (0, 1))
-        clip_unit(0)
+        clip_out(0, (3,))
+        clip_unit(0, (0, 1))
         interleave_gpsimd(0)
+        task_vectors(1)
+        copy_out(1, (0, 1))
         clip_out(1, (2, 3))
-        turn_x(0)
-        turn_x(1)
+        task_vectors(2)
+        copy_out(2, (0, 1))
+        clip_out(2, (2, 3))
         interleave_scalar(0)
-        task_vectors(2, (0, 1))
-        clip_out(2, (0, 1))
-        turn_x(2)
-        turn_x(3)
-        quantize_x(0)
-        quantize_x(1)
-        quantize_x(2)
-        quantize_x(3)
+        for m in range(4):
+            turn_x(m)
         quantize(0)
+        for m in range(4):
+            quantize_x(m)
+        clip_unit(1, (0, 1))
         interleave_gpsimd(1)
-        task_vectors(2, (2, 3))
-        copy_out(2, (2, 3))
+        task_vectors(3)
+        clip_out(3)
         turn_x(4)
         turn_x(5)
         interleave_scalar(1)
-        turn_x(6)
-        turn_x(7)
-        task_vectors(3)
-        clip_out(3)
         quantize(1)
         quantize_x(4)
         quantize_x(5)
-        clip_unit(2, (2, 3))
+        clip_unit(2, (0, 1))
         interleave_gpsimd(2)
         for m in range(4):
             base(0, m)
@@ -340,6 +334,9 @@ def tile_clipped_task_arithmetic_s4_kernel(
             if step > 0:
                 task_vectors(step + 3)
                 copy_out(step + 3)
+            else:
+                turn_x(6)
+                turn_x(7)
             interleave_scalar(step + 2)
             before = 2 if step < 4 else 1
             for n in range(4):

@@ -19,13 +19,20 @@ ACT = mybir.ActivationFunctionType
 FLOPS = 2 * M * K * N * (1 + T) + 2 * T * R * K * N
 
 P = 128
+PACK = 4
+KP = P * PACK
 NH = 512
 MT = M // P
-G = K // 512
+G = K // KP
 H = N // NH
 UNITS = H * T * G
+TILES = 4
+AHEAD = 3
 GP_COLS = 384
+GP_COLS_LAST = NH // 2
+EARLY_FROM = 3
 WARM_N = 256
+WARM_PASSES = 7
 
 
 def tile_clipped_task_arithmetic_s4_kernel(
@@ -39,17 +46,15 @@ def tile_clipped_task_arithmetic_s4_kernel(
         ctx.enter_context(tc.manual_schedule())
 
         u_raw = [keep.tile([P, 2 * K], U8, name=f"u_raw{i}", align_bytes=64) for i in range(T)]
-        u_ord = [[keep.tile([P, 4, 2 * P], U8, name=f"u_ord{i}_{g}", align_bytes=64) for g in range(G)] for i in range(T)]
+        u_ord = [[keep.tile([P, PACK, 2 * P], U8, name=f"u_ord{i}_{g}", align_bytes=64) for g in range(G)] for i in range(T)]
         us_raw = keep.tile([P, T * K], U8, name="us_raw", align_bytes=64)
-        us_ord = [[keep.tile([P, 4, P], U8, name=f"us_ord{i}_{g}", align_bytes=64) for g in range(G)] for i in range(T)]
+        us_ord = [[keep.tile([P, PACK, P], U8, name=f"us_ord{i}_{g}", align_bytes=64) for g in range(G)] for i in range(T)]
         v_sb = [[keep.tile([P, 2 * NH], U8, name=f"v{i}_{h}", align_bytes=64) for h in range(H)] for i in range(T)]
         vs_sb = keep.tile([P, T * N], U8, name="vs_sb", align_bytes=64)
         w_sb = [keep.tile([P, G, NH], I32, name=f"w{h}", align_bytes=64) for h in range(H)]
         ws_sb = keep.tile([P, H, G, NH], U8, name="ws_sb", align_bytes=64)
-        x_loads = ((0, 2), (2, 4), (4, 6), (6, 8))
-        x_sb = [keep.tile([P, b - a, K], BF16, name=f"x{a}", align_bytes=64) for a, b in x_loads]
-        x_row = [x_sb[c][:, m - a, :] for c, (a, b) in enumerate(x_loads) for m in range(a, b)]
-        xg = [keep.tile([P, G, P, 4], BF16, name=f"xg{m}", align_bytes=64) for m in range(MT)]
+        x_sb = [keep.tile([P, 2, K], BF16, name=f"x{c}", align_bytes=64) for c in range(MT // 2)]
+        xg = [keep.tile([P, G, P, PACK], BF16, name=f"xg{m}", align_bytes=64) for m in range(MT)]
         xq = [keep.tile([P, G, P], U32, name=f"xq{m}", align_bytes=64) for m in range(MT)]
         xs = [keep.tile([P, G, P], U8, name=f"xs{m}", align_bytes=64) for m in range(MT)]
         cq = [keep.tile([P, NH], U32, name=f"cq{j}", align_bytes=64) for j in range(UNITS)]
@@ -58,14 +63,15 @@ def tile_clipped_task_arithmetic_s4_kernel(
         warm_q = keep.tile([P, WARM_N], U32, name="warm_q", align_bytes=64)
         warm_s = keep.tile([P, WARM_N], U8, name="warm_s", align_bytes=64)
         ident = keep.tile([P, P], F32, name="ident")
-        lim_rows = keep.tile([P, 512], BF16, name="lim_rows")
-        lim_hi = keep.tile([P, T * G, 4], BF16, name="lim_hi")
-        lim_lo = keep.tile([P, T * G, 4], BF16, name="lim_lo")
+        lim_rows = keep.tile([P, KP], BF16, name="lim_rows")
+        lim_hi = keep.tile([P, T * G, PACK], BF16, name="lim_hi")
+        lim_lo = keep.tile([P, T * G, PACK], BF16, name="lim_lo")
         lam_sb = keep.tile([P, MT * T], BF16, name="lam_sb")
         lam_f = keep.tile([P, MT * T], F32, name="lam_f")
 
         x_view = x.rearrange("(p m) k -> p m k", m=MT)
         out_view = out.rearrange("(p m) n -> m p n", m=MT)
+        ws_rows = w_scales.rearrange("g r (h n) -> r h g n", h=H)
 
         def load_u(i):
             nc.sync.dma_start(out=u_raw[i][:].bitcast(I32), in_=u_words[0, :, 2 * K * i : 2 * K * (i + 1)].bitcast(I32))
@@ -78,10 +84,8 @@ def tile_clipped_task_arithmetic_s4_kernel(
             for q in range(4):
                 nc.sync.dma_start(out=plane[32 * q : 32 * q + 4].bitcast(I32), in_=rows[4 * q : 4 * q + 4].bitcast(I32))
 
-        ws_rows = w_scales.rearrange("g r (h n) -> r h g n", h=H)
-
         def load_x(c):
-            nc.sync.dma_start(out=x_sb[c][:], in_=x_view[:, x_loads[c][0] : x_loads[c][1], :])
+            nc.sync.dma_start(out=x_sb[c][:], in_=x_view[:, 2 * c : 2 * c + 2, :])
 
         def load_w(h):
             words = w_words.rearrange("g p n t -> p g (n t)").bitcast(I32)
@@ -103,9 +107,9 @@ def tile_clipped_task_arithmetic_s4_kernel(
         load_v(1, 0)
         load_x(0)
         load_x(1)
-        load_x(2)
         load_scale_rows(ws_sb[:, 0], ws_rows[:, 0])
         load_w(0)
+        load_x(2)
         load_x(3)
         nc.sync.dma_start(out=lam_sb[:], in_=lam.rearrange("(p m) i -> p (m i)", m=MT))
         load_v(0, 1)
@@ -115,25 +119,21 @@ def tile_clipped_task_arithmetic_s4_kernel(
 
         units = [(h, i, g) for h in range(H) for i in range(T) for g in range(G)]
 
-        def order_u(i, g):
-            order_u_codes(i, g)
-            order_u_scales(i, g)
-
         def order_u_codes(i, g):
             nc.vector.tensor_copy(
                 out=u_ord[i][g][:].bitcast(U16),
-                in_=u_raw[i][:, 1024 * g : 1024 * (g + 1)].bitcast(U16).rearrange("p (m t) -> p t m", t=4),
+                in_=u_raw[i][:, 2 * KP * g : 2 * KP * (g + 1)].bitcast(U16).rearrange("p (m t) -> p t m", t=PACK),
             )
 
         def order_u_scales(i, g):
             nc.vector.tensor_copy(
                 out=us_ord[i][g][:],
-                in_=us_raw[:, K * i + 512 * g : K * i + 512 * (g + 1)].rearrange("p (m t) -> p t m", t=4),
+                in_=us_raw[:, K * i + KP * g : K * i + KP * (g + 1)].rearrange("p (m t) -> p t m", t=PACK),
             )
 
-        def warm_up(passes):
+        def warm_up():
             ps = psum.tile([P, NH], F32, name="ps")
-            for r in range(passes):
+            for r in range(WARM_PASSES):
                 nc.tensor.matmul_mx(
                     out=ps[:, 0:WARM_N],
                     lhsT=warm_q[:, 0:P].bitcast(E4M3),
@@ -144,18 +144,34 @@ def tile_clipped_task_arithmetic_s4_kernel(
                     stop=True,
                 )
 
-        def turn_limits_mm():
+        def turn_limits():
             ps = psum.tile([P, 2, P], F32, name="ps")
             words = lim_rows[:].bitcast(F32)
             for u in range(2):
                 nc.tensor.transpose(ps[:, u, :], words[:, u::2], ident[:])
             nc.scalar.copy(out=lim_hi[:].bitcast(F32), in_=ps[:, :, 0 : T * G].rearrange("p u r -> p r u"))
 
-        def turn_limits_neg():
+        def negate_limits():
             nc.vector.tensor_scalar(out=lim_lo[:], in0=lim_hi[:], scalar1=-1.0, scalar2=None, op0=ALU.mult)
 
+        d_ps = {}
         d_sb = {}
         grp = {}
+
+        def task_vectors(j):
+            h, i, g = units[j]
+            d_sb[j] = work.tile([P, PACK, NH], BF16, name="d_sb", align_bytes=64)
+            for t in range(PACK):
+                d_ps[j, t] = psum.tile([P, NH], F32, name="ps")
+                nc.tensor.matmul_mx(
+                    out=d_ps[j, t][:],
+                    lhsT=u_ord[i][g][:, t, :].bitcast(E2M1),
+                    lhsT_scale=us_ord[i][g][:, t, :],
+                    rhs=v_sb[i][h][:].bitcast(E2M1),
+                    rhs_scale=vs_sb[:, N * i + NH * h : N * i + NH * (h + 1)],
+                    start=True,
+                    stop=True,
+                )
 
         def clip(j, t, src):
             h, i, g = units[j]
@@ -168,43 +184,24 @@ def tile_clipped_task_arithmetic_s4_kernel(
                 op1=ALU.max,
             )
 
-        d_ps = {}
-
-        def task_vectors(j, ts=range(4)):
-            h, i, g = units[j]
-            if j not in d_sb:
-                d_sb[j] = work.tile([P, 4, NH], BF16, name="d_sb", align_bytes=64)
-            for t in ts:
-                d_ps[j, t] = psum.tile([P, NH], F32, name="ps")
-                nc.tensor.matmul_mx(
-                    out=d_ps[j, t][:],
-                    lhsT=u_ord[i][g][:, t, :].bitcast(E2M1),
-                    lhsT_scale=us_ord[i][g][:, t, :],
-                    rhs=v_sb[i][h][:].bitcast(E2M1),
-                    rhs_scale=vs_sb[:, N * i + NH * h : N * i + NH * (h + 1)],
-                    start=True,
-                    stop=True,
-                )
-
-        def copy_out(j, ts=range(4)):
-            for t in ts:
+        def copy_out(j, slots):
+            for t in slots:
                 nc.scalar.copy(out=d_sb[j][:, t, :], in_=d_ps[j, t][:])
 
-        def clip_out(j, ts=range(4)):
-            for t in ts:
-                clip(j, t, d_ps[j, t][:])
-
-        def clip_unit(j, ts=range(4)):
-            for t in ts:
+        def clip_in_place(j, slots):
+            for t in slots:
                 clip(j, t, d_sb[j][:, t, :])
 
-        def four_by_four(j, c0, c1):
-            dst = grp[j][:, c0:c1, :].rearrange("p (c i) t -> p c t i", i=4)
-            src = d_sb[j][:, :, c0:c1].rearrange("p t (c i) -> p c t i", i=4)
-            return dst, src
+        def clip_out(j, slots):
+            for t in slots:
+                clip(j, t, d_ps[j, t][:])
 
-        def interleave_gpsimd(j, cols=GP_COLS):
-            grp[j] = keep.tile([P, NH, 4], BF16, name="grp", align_bytes=64)
+        def gpsimd_cols(j):
+            return GP_COLS if j < UNITS - 1 else GP_COLS_LAST
+
+        def interleave_gpsimd(j):
+            cols = gpsimd_cols(j)
+            grp[j] = keep.tile([P, NH, PACK], BF16, name="grp", align_bytes=64)
             nc.gpsimd.tensor_scalar(
                 out=grp[j][:, 0:cols, :],
                 in0=d_sb[j][:, :, 0:cols].rearrange("p t n -> p n t"),
@@ -214,19 +211,22 @@ def tile_clipped_task_arithmetic_s4_kernel(
                 op1=ALU.add,
             )
 
-        def interleave_scalar(j, first=GP_COLS):
-            dst, src = four_by_four(j, first, NH)
-            nc.scalar.copy(out=dst, in_=src)
+        def interleave_scalar(j):
+            cols = gpsimd_cols(j)
+            nc.scalar.copy(
+                out=grp[j][:, cols:NH, :].rearrange("p (c i) t -> p c t i", i=4),
+                in_=d_sb[j][:, :, cols:NH].rearrange("p t (c i) -> p c t i", i=4),
+            )
 
-        def quantize(j):
+        def quantize_unit(j):
             nc.vector.quantize_mx(out=cq[j][:].bitcast(E4M3), scales=cs[j][:], in_=grp[j][:].rearrange("p n t -> p (n t)"))
 
         def turn_x(m):
             ps = psum.tile([P, G, 2, P], F32, name="ps")
-            words = x_row[m].bitcast(F32)
+            words = x_sb[m // 2][:, m % 2, :].bitcast(F32)
             for g in range(G):
                 for u in range(2):
-                    nc.tensor.transpose(ps[:, g, u, :], words[:, 256 * g + u : 256 * (g + 1) : 2], ident[:])
+                    nc.tensor.transpose(ps[:, g, u, :], words[:, 2 * P * g + u : 2 * P * (g + 1) : 2], ident[:])
             nc.scalar.copy(out=xg[m][:].bitcast(F32), in_=ps[:].rearrange("p g u n -> p g n u"))
 
         def quantize_x(m):
@@ -236,35 +236,35 @@ def tile_clipped_task_arithmetic_s4_kernel(
                 in_=xg[m][:].rearrange("p g n t -> p (g n t)"),
             )
 
-        def x_pass(ps, m, g, rhs, rhs_scale, cols):
-            nc.tensor.matmul_mx(
-                out=ps[:, cols],
-                lhsT=xq[m][:, g, :].bitcast(E4M3),
-                lhsT_scale=xs[m][:, g, :],
-                rhs=rhs[:, cols].bitcast(E4M3),
-                rhs_scale=rhs_scale[:, cols],
-                start=(g == 0),
-                stop=(g == G - 1),
-            )
-
-        def base(h, m):
+        def x_times(m, codes, scales, cols):
             ps = psum.tile([P, NH], F32, name="ps")
             for g in range(G):
-                x_pass(ps, m, g, w_sb[h][:, g, :], ws_sb[:, h, g, :], slice(0, NH))
-            nc.scalar.copy(out=acc[h][m][:], in_=ps[:])
+                nc.tensor.matmul_mx(
+                    out=ps[:, cols],
+                    lhsT=xq[m][:, g, :].bitcast(E4M3),
+                    lhsT_scale=xs[m][:, g, :],
+                    rhs=codes[g][:, cols].bitcast(E4M3),
+                    rhs_scale=scales[g][:, cols],
+                    start=(g == 0),
+                    stop=(g == G - 1),
+                )
+            return ps
 
-        z_ps = {}
+        def base_product(h, m):
+            return x_times(m, [w_sb[h][:, g, :] for g in range(G)], [ws_sb[:, h, g, :] for g in range(G)], slice(0, NH))
 
-        def task_pass(pair, m, g, cols=slice(0, NH)):
-            if g == 0:
-                z_ps[pair, m] = psum.tile([P, NH], F32, name="ps")
-            x_pass(z_ps[pair, m], m, g, cq[G * pair + g], cs[G * pair + g], cols)
+        def base(h, m):
+            nc.scalar.copy(out=acc[h][m][:], in_=base_product(h, m)[:])
 
-        def add_task(pair, m, cols=slice(0, NH)):
+        def task_product(pair, m, cols):
+            return x_times(m, cq[G * pair : G * (pair + 1)], cs[G * pair : G * (pair + 1)], cols)
+
+        def task(pair, m, cols=slice(0, NH)):
             h, i = divmod(pair, T)
+            ps = task_product(pair, m, cols)
             nc.vector.scalar_tensor_tensor(
                 out=acc[h][m][:, cols],
-                in0=z_ps[pair, m][:, cols],
+                in0=ps[:, cols],
                 scalar=lam_sb[:, m * T + i : m * T + i + 1],
                 in1=acc[h][m][:, cols],
                 op0=ALU.mult,
@@ -273,92 +273,92 @@ def tile_clipped_task_arithmetic_s4_kernel(
             if i == T - 1:
                 nc.sync.dma_start(out=out_view[m][:, NH * h + cols.start : NH * h + cols.stop], in_=acc[h][m][:, cols])
 
-        def task_beside(pair, m):
+        def task_beside_vector(pair, m):
             h, i = divmod(pair, T)
-            for g in range(G):
-                task_pass(pair, m, g)
+            ps = task_product(pair, m, slice(0, NH))
             part = work.tile([P, NH], F32, name="part", align_bytes=64)
-            nc.scalar.activation(out=part[:], in_=z_ps[pair, m][:], func=ACT.Copy, scale=lam_f[:, m * T + i : m * T + i + 1])
+            nc.scalar.activation(out=part[:], in_=ps[:], func=ACT.Copy, scale=lam_f[:, m * T + i : m * T + i + 1])
             nc.gpsimd.tensor_tensor(out=acc[h][m][:], in0=acc[h][m][:], in1=part[:], op=ALU.add)
 
-        def task(pair, m, cols=slice(0, NH)):
-            for g in range(G):
-                task_pass(pair, m, g, cols)
-            add_task(pair, m, cols)
-
-        warm_up(7)
-        order_u(0, 0)
-        order_u(0, 1)
+        first_slots, last_slots, all_slots = (0, 1), (2, 3), range(PACK)
+        warm_up()
+        for g in range(G):
+            order_u_codes(0, g)
+            order_u_scales(0, g)
         for g in range(G):
             order_u_scales(1, g)
-        turn_limits_mm()
+        turn_limits()
         task_vectors(0)
-        copy_out(0, (0, 1))
-        turn_limits_neg()
-        clip_out(0, (2,))
+        copy_out(0, first_slots)
+        negate_limits()
         for g in range(G):
+            clip_out(0, (last_slots[g],))
             order_u_codes(1, g)
-        clip_out(0, (3,))
-        clip_unit(0, (0, 1))
+        clip_in_place(0, first_slots)
         interleave_gpsimd(0)
-        task_vectors(1)
-        copy_out(1, (0, 1))
-        clip_out(1, (2, 3))
-        task_vectors(2)
-        copy_out(2, (0, 1))
-        clip_out(2, (2, 3))
+        for j in (1, 2):
+            task_vectors(j)
+            copy_out(j, first_slots)
+            clip_out(j, last_slots)
         interleave_scalar(0)
-        for m in range(4):
+        for m in range(TILES):
             turn_x(m)
-        quantize(0)
-        for m in range(4):
-            quantize_x(m)
-        clip_unit(1, (0, 1))
+        quantize_x(0)
+        quantize_x(1)
+        quantize_unit(0)
+        quantize_x(2)
+        quantize_x(3)
+        clip_in_place(1, first_slots)
         interleave_gpsimd(1)
         task_vectors(3)
-        clip_out(3)
+        clip_out(3, all_slots)
+        base(0, 0)
+        base(0, 1)
+        interleave_scalar(1)
+        base(0, 2)
+        waiting = base_product(0, 3)
         turn_x(4)
         turn_x(5)
-        interleave_scalar(1)
-        quantize(1)
+        nc.scalar.copy(out=acc[0][3][:], in_=waiting[:])
+        turn_x(6)
+        turn_x(7)
+        quantize_unit(1)
         quantize_x(4)
         quantize_x(5)
-        clip_unit(2, (0, 1))
+        clip_in_place(2, first_slots)
         interleave_gpsimd(2)
-        for m in range(4):
-            base(0, m)
-        last = H * T - 1
-        for step in range(UNITS - 3):
-            pair, half = divmod(step, 2)
-            tiles = range(4 * half, 4 * half + 4)
+
+        for step in range(UNITS - AHEAD):
+            pair, part_of_tiles = divmod(step, MT // TILES)
+            unit = step + AHEAD
             if step > 0:
-                task_vectors(step + 3)
-                copy_out(step + 3)
-            else:
-                turn_x(6)
-                turn_x(7)
-            interleave_scalar(step + 2)
-            before = 2 if step < 4 else 1
-            for n in range(4):
-                if n == before:
+                task_vectors(unit)
+                copy_out(unit, all_slots)
+            interleave_scalar(unit - 1)
+            adds_before = 2 if step < EARLY_FROM else 1
+            for n in range(TILES):
+                if n == adds_before:
                     if step == 0:
                         quantize_x(6)
                         quantize_x(7)
-                        nc.vector.tensor_copy(out=lam_f[:], in_=lam_sb[:])
                     else:
-                        clip_unit(step + 3)
-                    quantize(step + 2)
-                    interleave_gpsimd(step + 3, GP_COLS if step + 4 < UNITS else NH // 2)
-                task(pair, tiles[n])
+                        clip_in_place(unit, all_slots)
+                    quantize_unit(unit - 1)
+                    interleave_gpsimd(unit)
+                    if step == 1:
+                        nc.gpsimd.tensor_copy(out=lam_f[:], in_=lam_sb[:])
+                task(pair, TILES * part_of_tiles + n)
                 if n < 2:
-                    base(*divmod(4 + 2 * step + n, MT))
-        interleave_scalar(UNITS - 1, NH // 2)
+                    base(*divmod(TILES + 2 * step + n, MT))
+
+        last = H * T - 1
+        interleave_scalar(UNITS - 1)
         task(last - 1, MT - 4)
-        base(1, MT - 2)
-        quantize(UNITS - 1)
+        base(H - 1, MT - 2)
+        quantize_unit(UNITS - 1)
         task(last - 1, MT - 3)
-        base(1, MT - 1)
-        task_beside(last - 1, MT - 2)
+        base(H - 1, MT - 1)
+        task_beside_vector(last - 1, MT - 2)
         for m in range(MT - 1):
             task(last, m)
         for pair in (last - 1, last):

@@ -63,7 +63,6 @@ def tile_clipped_task_arithmetic_s4_kernel(
         warm_q = keep.tile([P, WARM_N], U32, name="warm_q", align_bytes=64)
         warm_s = keep.tile([P, WARM_N], U8, name="warm_s", align_bytes=64)
         ident = keep.tile([P, P], F32, name="ident")
-        lim_rows = keep.tile([P, KP], BF16, name="lim_rows")
         lim_hi = keep.tile([P, T * G, PACK], BF16, name="lim_hi")
         lim_lo = keep.tile([P, T * G, PACK], BF16, name="lim_lo")
         lam_sb = keep.tile([P, MT * T], BF16, name="lam_sb")
@@ -91,18 +90,18 @@ def tile_clipped_task_arithmetic_s4_kernel(
             words = w_words.rearrange("g p n t -> p g (n t)").bitcast(I32)
             nc.sync.dma_start(out=w_sb[h][:], in_=words[:, :, NH * h : NH * (h + 1)])
 
-        nc.vector.memset(lim_rows[:].bitcast(I32), 0)
         nc.vector.memset(us_raw[:].bitcast(I32), 0)
         nc.vector.memset(vs_sb[:].bitcast(I32), 0)
         ws_flat = ws_sb[:].rearrange("p h g n -> p (h g n)")
         nc.vector.memset(ws_flat.bitcast(I32), 0)
-        nc.gpsimd.dma_start(out=lim_rows[0 : T * G, :], in_=lim.rearrange("i (g c) -> (i g) c", g=G))
         make_identity(nc, ident[:])
         nc.vector.quantize_mx(out=warm_q[:].bitcast(E4M3), scales=warm_s[:], in_=ws_flat.bitcast(BF16))
         load_v(0, 0)
         load_u(0)
         load_scale_rows(us_raw, u_scales[0])
         load_scale_rows(vs_sb, v_scales[0])
+        with nc.allow_non_contiguous_dma(reason="four limits a partition and row"):
+            nc.sync.dma_start(out=lim_hi[:], in_=lim.rearrange("i (g p t) -> p (i g) t", g=G, t=PACK))
         load_u(1)
         load_v(1, 0)
         load_x(0)
@@ -143,13 +142,6 @@ def tile_clipped_task_arithmetic_s4_kernel(
                     start=True,
                     stop=True,
                 )
-
-        def turn_limits():
-            ps = psum.tile([P, 2, P], F32, name="ps")
-            words = lim_rows[:].bitcast(F32)
-            for u in range(2):
-                nc.tensor.transpose(ps[:, u, :], words[:, u::2], ident[:])
-            nc.scalar.copy(out=lim_hi[:].bitcast(F32), in_=ps[:, :, 0 : T * G].rearrange("p u r -> p r u"))
 
         def negate_limits():
             nc.vector.tensor_scalar(out=lim_lo[:], in0=lim_hi[:], scalar1=-1.0, scalar2=None, op0=ALU.mult)
@@ -287,7 +279,6 @@ def tile_clipped_task_arithmetic_s4_kernel(
             order_u_scales(0, g)
         for g in range(G):
             order_u_scales(1, g)
-        turn_limits()
         task_vectors(0)
         copy_out(0, first_slots)
         negate_limits()

@@ -31,6 +31,7 @@ AHEAD = 3
 GP_COLS = 384
 GP_COLS_LAST = NH // 2
 EARLY_FROM = 3
+SHORT_STEP = 3
 WARM_N = 256
 WARM_PASSES = 7
 
@@ -251,7 +252,7 @@ def tile_clipped_task_arithmetic_s4_kernel(
         def task_product(pair, m, cols):
             return x_times(m, cq[G * pair : G * (pair + 1)], cs[G * pair : G * (pair + 1)], cols)
 
-        def task(pair, m, cols=slice(0, NH)):
+        def task(pair, m, cols=slice(0, NH), stored=None):
             h, i = divmod(pair, T)
             ps = task_product(pair, m, cols)
             nc.vector.scalar_tensor_tensor(
@@ -262,8 +263,9 @@ def tile_clipped_task_arithmetic_s4_kernel(
                 op0=ALU.mult,
                 op1=ALU.add,
             )
-            if i == T - 1:
-                nc.sync.dma_start(out=out_view[m][:, NH * h + cols.start : NH * h + cols.stop], in_=acc[h][m][:, cols])
+            if i == T - 1 and (stored is None or stored.stop == cols.stop):
+                stored = stored or cols
+                nc.sync.dma_start(out=out_view[m][:, NH * h + stored.start : NH * h + stored.stop], in_=acc[h][m][:, stored])
 
         def task_beside_vector(pair, m):
             h, i = divmod(pair, T)
@@ -319,6 +321,7 @@ def tile_clipped_task_arithmetic_s4_kernel(
         clip_in_place(2, first_slots)
         interleave_gpsimd(2)
 
+        bases = [divmod(b, MT) for b in range(TILES, H * MT)]
         for step in range(UNITS - AHEAD):
             pair, part_of_tiles = divmod(step, MT // TILES)
             unit = step + AHEAD
@@ -339,19 +342,24 @@ def tile_clipped_task_arithmetic_s4_kernel(
                     if step == 1:
                         nc.gpsimd.tensor_copy(out=lam_f[:], in_=lam_sb[:])
                 task(pair, TILES * part_of_tiles + n)
-                if n < 2:
-                    base(*divmod(TILES + 2 * step + n, MT))
+                if n < (1 if step == SHORT_STEP else 2):
+                    base(*bases.pop(0))
 
         last = H * T - 1
+        halves = (slice(0, NH // 2), slice(NH // 2, NH))
         interleave_scalar(UNITS - 1)
+        base(H - 1, MT - 3)
         task(last - 1, MT - 4)
         base(H - 1, MT - 2)
         quantize_unit(UNITS - 1)
         task(last - 1, MT - 3)
-        base(H - 1, MT - 1)
         task_beside_vector(last - 1, MT - 2)
-        for m in range(MT - 1):
+        for m in range(MT - 2):
             task(last, m)
-        for pair in (last - 1, last):
-            task(pair, MT - 1, slice(0, NH // 2))
-            task(pair, MT - 1, slice(NH // 2, NH))
+        base(H - 1, MT - 1)
+        for cols in halves:
+            task(last, MT - 2, cols, slice(0, NH))
+        for cols in halves:
+            task(last - 1, MT - 1, cols)
+        for cols in (halves[0], slice(NH // 2, 3 * NH // 4), slice(3 * NH // 4, NH)):
+            task(last, MT - 1, cols)

@@ -80,9 +80,9 @@ def tile_clipped_task_arithmetic_s4_kernel(
             c0 = 2 * (N * i + NH * h)
             nc.sync.dma_start(out=v_sb[i][h][:].bitcast(I32), in_=v_words[0, :, c0 : c0 + 2 * NH].bitcast(I32))
 
-        def load_scale_rows(plane, rows):
-            for q in range(4):
-                nc.sync.dma_start(out=plane[32 * q : 32 * q + 4].bitcast(I32), in_=rows[4 * q : 4 * q + 4].bitcast(I32))
+        def load_scale_rows(plane, rows, quadrants=range(4), queue=nc.sync):
+            for q in quadrants:
+                queue.dma_start(out=plane[32 * q : 32 * q + 4].bitcast(I32), in_=rows[4 * q : 4 * q + 4].bitcast(I32))
 
         def load_x(c):
             nc.sync.dma_start(out=x_sb[c][:], in_=x_view[:, 2 * c : 2 * c + 2, :])
@@ -91,16 +91,18 @@ def tile_clipped_task_arithmetic_s4_kernel(
             words = w_words.rearrange("g p n t -> p g (n t)").bitcast(I32)
             nc.sync.dma_start(out=w_sb[h][:], in_=words[:, :, NH * h : NH * (h + 1)])
 
-        nc.vector.memset(us_raw[:].bitcast(I32), 0)
-        nc.vector.memset(vs_sb[:].bitcast(I32), 0)
         ws_flat = ws_sb[:].rearrange("p h g n -> p (h g n)")
         nc.vector.memset(ws_flat.bitcast(I32), 0)
+        nc.vector.memset(vs_sb[:].bitcast(I32), 0)
+        nc.vector.memset(us_raw[:].bitcast(I32), 0)
+        load_scale_rows(vs_sb, v_scales[0], (3,), nc.gpsimd)
         make_identity(nc, ident[:])
         nc.vector.quantize_mx(out=warm_q[:].bitcast(E4M3), scales=warm_s[:], in_=ws_flat.bitcast(BF16))
         load_v(0, 0)
         load_u(0)
+        load_scale_rows(vs_sb, v_scales[0], (0, 2))
         load_scale_rows(us_raw, u_scales[0])
-        load_scale_rows(vs_sb, v_scales[0])
+        load_scale_rows(vs_sb, v_scales[0], (1,))
         with nc.allow_non_contiguous_dma(reason="four limits a partition and row"):
             nc.sync.dma_start(out=lim_hi[:], in_=lim.rearrange("i (g p t) -> p (i g) t", g=G, t=PACK))
         load_u(1)

@@ -56,6 +56,7 @@ def tile_clipped_task_arithmetic_s4_kernel(
         ws_sb = keep.tile([P, H, G, NH], U8, name="ws_sb", align_bytes=64)
         x_sb = [keep.tile([P, 2, K], BF16, name=f"x{c}", align_bytes=64) for c in range(MT // 2)]
         xg = [keep.tile([P, G, P, PACK], BF16, name=f"xg{m}", align_bytes=64) for m in range(MT)]
+        x_sorted = {m: keep.tile([P, 2, G * P], F32, name=f"x_sorted{m}", align_bytes=64) for m in range(TILES, MT)}
         xq = [keep.tile([P, G, P], U32, name=f"xq{m}", align_bytes=64) for m in range(MT)]
         xs = [keep.tile([P, G, P], U8, name=f"xs{m}", align_bytes=64) for m in range(MT)]
         cq = [keep.tile([P, NH], U32, name=f"cq{j}", align_bytes=64) for j in range(UNITS)]
@@ -105,8 +106,7 @@ def tile_clipped_task_arithmetic_s4_kernel(
         load_scale_rows(vs_sb, v_scales[0], (1,))
         with nc.allow_non_contiguous_dma(reason="four limits a partition and row"):
             nc.sync.dma_start(out=lim_hi[:], in_=lim.rearrange("i (g p t) -> p (i g) t", g=G, t=PACK))
-        load_u(1)
-        load_v(1, 0)
+        load_v(0, 1)
         load_x(0)
         load_x(1)
         load_scale_rows(ws_sb[:, 0], ws_rows[:, 0])
@@ -114,12 +114,13 @@ def tile_clipped_task_arithmetic_s4_kernel(
         load_x(2)
         load_x(3)
         nc.sync.dma_start(out=lam_sb[:], in_=lam.rearrange("(p m) i -> p (m i)", m=MT))
-        load_v(0, 1)
+        load_u(1)
         load_w(1)
         load_scale_rows(ws_sb[:, 1], ws_rows[:, 1])
+        load_v(1, 0)
         load_v(1, 1)
 
-        units = [(h, i, g) for h in range(H) for i in range(T) for g in range(G)]
+        units = [(h, i, g) for i in range(T) for h in range(H) for g in range(G)]
 
         def order_u_codes(i, g):
             nc.vector.tensor_copy(
@@ -192,7 +193,7 @@ def tile_clipped_task_arithmetic_s4_kernel(
                 clip(j, t, d_ps[j, t][:])
 
         def gpsimd_cols(j):
-            return GP_COLS if j < UNITS - 1 else GP_COLS_LAST
+            return NH if j == 0 else GP_COLS if j < 3 else 320 if j < UNITS - 1 else GP_COLS_LAST
 
         def interleave_gpsimd(j):
             cols = gpsimd_cols(j)
@@ -216,12 +217,19 @@ def tile_clipped_task_arithmetic_s4_kernel(
         def quantize_unit(j):
             nc.vector.quantize_mx(out=cq[j][:].bitcast(E4M3), scales=cs[j][:], in_=grp[j][:].rearrange("p n t -> p (n t)"))
 
+        def sort_x(m):
+            words = x_sb[m // 2][:, m % 2, :].bitcast(F32)
+            nc.scalar.copy(out=x_sorted[m][:], in_=words.rearrange("p (w u) -> p u w", u=2))
+
         def turn_x(m):
             ps = psum.tile([P, G, 2, P], F32, name="ps")
             words = x_sb[m // 2][:, m % 2, :].bitcast(F32)
             for g in range(G):
                 for u in range(2):
-                    nc.tensor.transpose(ps[:, g, u, :], words[:, 2 * P * g + u : 2 * P * (g + 1) : 2], ident[:])
+                    if m in x_sorted:
+                        nc.tensor.transpose(ps[:, g, u, :], x_sorted[m][:, u, P * g : P * (g + 1)], ident[:])
+                    else:
+                        nc.tensor.transpose(ps[:, g, u, :], words[:, 2 * P * g + u : 2 * P * (g + 1) : 2], ident[:])
             nc.scalar.copy(out=xg[m][:].bitcast(F32), in_=ps[:].rearrange("p g u n -> p g n u"))
 
         def quantize_x(m):
@@ -251,11 +259,14 @@ def tile_clipped_task_arithmetic_s4_kernel(
         def base(h, m):
             nc.scalar.copy(out=acc[h][m][:], in_=base_product(h, m)[:])
 
+        def base_on_vector(h, m):
+            nc.vector.tensor_copy(out=acc[h][m][:], in_=base_product(h, m)[:])
+
         def task_product(pair, m, cols):
             return x_times(m, cq[G * pair : G * (pair + 1)], cs[G * pair : G * (pair + 1)], cols)
 
         def task(pair, m, cols=slice(0, NH), stored=None):
-            h, i = divmod(pair, T)
+            i, h = divmod(pair, H)
             ps = task_product(pair, m, cols)
             nc.vector.scalar_tensor_tensor(
                 out=acc[h][m][:, cols],
@@ -270,7 +281,7 @@ def tile_clipped_task_arithmetic_s4_kernel(
                 nc.sync.dma_start(out=out_view[m][:, NH * h + stored.start : NH * h + stored.stop], in_=acc[h][m][:, stored])
 
         def task_beside_vector(pair, m):
-            h, i = divmod(pair, T)
+            i, h = divmod(pair, H)
             ps = task_product(pair, m, slice(0, NH))
             part = work.tile([P, NH], F32, name="part", align_bytes=64)
             nc.scalar.activation(out=part[:], in_=ps[:], func=ACT.Copy, scale=lam_f[:, m * T + i : m * T + i + 1])
@@ -281,21 +292,16 @@ def tile_clipped_task_arithmetic_s4_kernel(
         for g in range(G):
             order_u_codes(0, g)
             order_u_scales(0, g)
-        for g in range(G):
-            order_u_scales(1, g)
-        task_vectors(0)
-        copy_out(0, first_slots)
         negate_limits()
-        for g in range(G):
-            clip_out(0, (last_slots[g],))
-            order_u_codes(1, g)
-        clip_in_place(0, first_slots)
-        interleave_gpsimd(0)
-        for j in (1, 2):
+        order_u_scales(1, 0)
+        order_u_scales(1, 1)
+        for j in range(4):
             task_vectors(j)
             copy_out(j, first_slots)
             clip_out(j, last_slots)
-        interleave_scalar(0)
+            if j == 0:
+                clip_in_place(0, first_slots)
+                interleave_gpsimd(0)
         for m in range(TILES):
             turn_x(m)
         quantize_x(0)
@@ -305,63 +311,72 @@ def tile_clipped_task_arithmetic_s4_kernel(
         quantize_x(3)
         clip_in_place(1, first_slots)
         interleave_gpsimd(1)
-        task_vectors(3)
-        clip_out(3, all_slots)
-        base(0, 0)
-        base(0, 1)
+        for m in range(TILES, MT):
+            sort_x(m)
         interleave_scalar(1)
-        base(0, 2)
-        waiting = base_product(0, 3)
-        turn_x(4)
-        turn_x(5)
-        nc.scalar.copy(out=acc[0][3][:], in_=waiting[:])
-        turn_x(6)
-        turn_x(7)
+        for m in range(TILES):
+            base_on_vector(0, m)
+        for m in range(TILES, MT):
+            turn_x(m)
         quantize_unit(1)
         quantize_x(4)
         quantize_x(5)
+        order_u_codes(1, 0)
         clip_in_place(2, first_slots)
         interleave_gpsimd(2)
+        nc.scalar.copy(out=lam_f[:], in_=lam_sb[:])
 
-        bases = [divmod(b, MT) for b in range(TILES, H * MT)]
-        for step in range(UNITS - AHEAD):
-            pair, part_of_tiles = divmod(step, MT // TILES)
+        B = "base"
+        steps = [
+            [(B, 1, 0), (B, 1, 1), (0, 0), (0, 1), (B, 0, 4), (0, 2), (0, 3)],
+            [(B, 0, 5), (0, 4), (B, 0, 6), (0, 5), (B, 0, 7)],
+            [(0, 6), (0, 7), (B, 1, 2), (1, 0), (1, 1)],
+            [(1, 2), (B, 1, 3), (B, 1, 4), (1, 3), (1, 4)],
+            [(2, 0), (2, 1), (B, 1, 5), (2, 2), (B, 1, 6), (2, 3)],
+        ]
+        scalar_slots = [first_slots, all_slots, (1, 2, 3), (1, 2, 3), all_slots]
+        inter_at = [2, 3, 0, 0, 0]
+        group_at = [7, 4, 3, 3, 2]
+        for step, products in enumerate(steps):
             unit = step + AHEAD
             if step > 0:
                 task_vectors(unit)
-                copy_out(unit, all_slots)
-            interleave_scalar(unit - 1)
-            adds_before = 2 if step < EARLY_FROM else 1
-            for n in range(TILES):
-                if n == adds_before:
+                copy_out(unit, scalar_slots[step])
+                clip_out(unit, [t for t in all_slots if t not in scalar_slots[step]])
+            for n, product in enumerate(products + [None]):
+                if n == inter_at[step]:
+                    interleave_scalar(unit - 1)
+                if n == group_at[step]:
                     if step == 0:
                         quantize_x(6)
                         quantize_x(7)
-                    else:
-                        clip_in_place(unit, all_slots)
+                        order_u_codes(1, 1)
+                    clip_in_place(unit, scalar_slots[step])
                     quantize_unit(unit - 1)
                     interleave_gpsimd(unit)
-                    if step == 1:
-                        nc.gpsimd.tensor_copy(out=lam_f[:], in_=lam_sb[:])
-                task(pair, TILES * part_of_tiles + n)
-                if n < (1 if step == SHORT_STEP else 2):
-                    base(*bases.pop(0))
+                if product is None:
+                    continue
+                if product[0] == B:
+                    base(*product[1:])
+                else:
+                    task(*product)
 
         last = H * T - 1
         halves = (slice(0, NH // 2), slice(NH // 2, NH))
         interleave_scalar(UNITS - 1)
-        base(H - 1, MT - 3)
-        task(last - 1, MT - 4)
-        base(H - 1, MT - 2)
+        task(2, 4)
         quantize_unit(UNITS - 1)
-        task(last - 1, MT - 3)
-        task_beside_vector(last - 1, MT - 2)
+        task(2, 5)
+        task_beside_vector(1, 5)
+        task(2, 6)
+        task(2, 7)
+        task_beside_vector(1, 6)
         for m in range(MT - 2):
             task(last, m)
         base(H - 1, MT - 1)
         for cols in halves:
             task(last, MT - 2, cols, slice(0, NH))
         for cols in halves:
-            task(last - 1, MT - 1, cols)
+            task(1, MT - 1, cols)
         for cols in (halves[0], slice(NH // 2, 3 * NH // 4), slice(3 * NH // 4, NH)):
             task(last, MT - 1, cols)

@@ -26,12 +26,11 @@ MT = M // P
 G = K // KP
 H = N // NH
 UNITS = H * T * G
-TILES = 4
-AHEAD = 3
-GP_COLS = 384
+EARLY = MT // 2
+FIRST_UNITS = H * G
+GP_COLS_WIDE = 384
+GP_COLS_STEP = 320
 GP_COLS_LAST = NH // 2
-EARLY_FROM = 3
-SHORT_STEP = 3
 WARM_N = 256
 WARM_PASSES = 7
 
@@ -56,7 +55,7 @@ def tile_clipped_task_arithmetic_s4_kernel(
         ws_sb = keep.tile([P, H, G, NH], U8, name="ws_sb", align_bytes=64)
         x_sb = [keep.tile([P, 2, K], BF16, name=f"x{c}", align_bytes=64) for c in range(MT // 2)]
         xg = [keep.tile([P, G, P, PACK], BF16, name=f"xg{m}", align_bytes=64) for m in range(MT)]
-        x_sorted = {m: keep.tile([P, 2, G * P], F32, name=f"x_sorted{m}", align_bytes=64) for m in range(TILES, MT)}
+        x_sorted = {m: keep.tile([P, 2, G * P], F32, name=f"x_sorted{m}", align_bytes=64) for m in range(EARLY, MT)}
         xq = [keep.tile([P, G, P], U32, name=f"xq{m}", align_bytes=64) for m in range(MT)]
         xs = [keep.tile([P, G, P], U8, name=f"xs{m}", align_bytes=64) for m in range(MT)]
         cq = [keep.tile([P, NH], U32, name=f"cq{j}", align_bytes=64) for j in range(UNITS)]
@@ -154,10 +153,11 @@ def tile_clipped_task_arithmetic_s4_kernel(
         d_sb = {}
         grp = {}
 
-        def task_vectors(j):
+        def task_vectors(j, slots=range(PACK)):
             h, i, g = units[j]
-            d_sb[j] = work.tile([P, PACK, NH], BF16, name="d_sb", align_bytes=64)
-            for t in range(PACK):
+            if j not in d_sb:
+                d_sb[j] = work.tile([P, PACK, NH], BF16, name="d_sb", align_bytes=64)
+            for t in slots:
                 d_ps[j, t] = psum.tile([P, NH], F32, name="ps")
                 nc.tensor.matmul_mx(
                     out=d_ps[j, t][:],
@@ -193,7 +193,11 @@ def tile_clipped_task_arithmetic_s4_kernel(
                 clip(j, t, d_ps[j, t][:])
 
         def gpsimd_cols(j):
-            return NH if j == 0 else GP_COLS if j < 3 else 320 if j < UNITS - 1 else GP_COLS_LAST
+            if j == 0:
+                return NH
+            if j == UNITS - 1:
+                return GP_COLS_LAST
+            return GP_COLS_STEP if FIRST_UNITS - 1 <= j < UNITS - 2 else GP_COLS_WIDE
 
         def interleave_gpsimd(j):
             cols = gpsimd_cols(j)
@@ -287,36 +291,53 @@ def tile_clipped_task_arithmetic_s4_kernel(
             nc.scalar.activation(out=part[:], in_=ps[:], func=ACT.Copy, scale=lam_f[:, m * T + i : m * T + i + 1])
             nc.gpsimd.tensor_tensor(out=acc[h][m][:], in0=acc[h][m][:], in1=part[:], op=ALU.add)
 
-        first_slots, last_slots, all_slots = (0, 1), (2, 3), range(PACK)
+        def sbuf_group(unit, slots):
+            clip_in_place(unit, slots)
+            quantize_unit(unit - 1)
+            interleave_gpsimd(unit)
+
+        def step_head(unit, scalar_slots):
+            task_vectors(unit)
+            copy_out(unit, scalar_slots)
+            clip_out(unit, [t for t in all_slots if t not in scalar_slots])
+
+        first_slots, last_slots, all_slots = (0, 1), (2, 3), tuple(range(PACK))
+        late_tiles = range(EARLY, MT)
+
         warm_up()
         for g in range(G):
             order_u_codes(0, g)
             order_u_scales(0, g)
         negate_limits()
-        order_u_scales(1, 0)
-        order_u_scales(1, 1)
-        for j in range(4):
+        for g in range(G):
+            order_u_scales(1, g)
+        for j in range(FIRST_UNITS - 1):
             task_vectors(j)
             copy_out(j, first_slots)
             clip_out(j, last_slots)
             if j == 0:
                 clip_in_place(0, first_slots)
                 interleave_gpsimd(0)
-        for m in range(TILES):
+        task_vectors(3, first_slots)
+        copy_out(3, first_slots)
+        for m in range(EARLY):
             turn_x(m)
         quantize_x(0)
-        quantize_x(1)
         quantize_unit(0)
+        quantize_x(1)
         quantize_x(2)
         quantize_x(3)
         clip_in_place(1, first_slots)
         interleave_gpsimd(1)
-        for m in range(TILES, MT):
+        task_vectors(3, last_slots)
+        clip_out(3, last_slots)
+        for m in late_tiles:
             sort_x(m)
         interleave_scalar(1)
-        for m in range(TILES):
+        for m in range(EARLY - 1):
             base_on_vector(0, m)
-        for m in range(TILES, MT):
+        base(0, EARLY - 1)
+        for m in late_tiles:
             turn_x(m)
         quantize_unit(1)
         quantize_x(4)
@@ -326,57 +347,75 @@ def tile_clipped_task_arithmetic_s4_kernel(
         interleave_gpsimd(2)
         nc.scalar.copy(out=lam_f[:], in_=lam_sb[:])
 
-        B = "base"
-        steps = [
-            [(B, 1, 0), (B, 1, 1), (0, 0), (0, 1), (B, 0, 4), (0, 2), (0, 3)],
-            [(B, 0, 5), (0, 4), (B, 0, 6), (0, 5), (B, 0, 7)],
-            [(0, 6), (0, 7), (B, 1, 2), (1, 0), (1, 1)],
-            [(1, 2), (B, 1, 3), (B, 1, 4), (1, 3), (1, 4)],
-            [(2, 0), (2, 1), (B, 1, 5), (2, 2), (B, 1, 6), (2, 3)],
-        ]
-        scalar_slots = [first_slots, all_slots, (1, 2, 3), (1, 2, 3), all_slots]
-        inter_at = [2, 3, 0, 0, 0]
-        group_at = [7, 4, 3, 3, 2]
-        for step, products in enumerate(steps):
-            unit = step + AHEAD
-            if step > 0:
-                task_vectors(unit)
-                copy_out(unit, scalar_slots[step])
-                clip_out(unit, [t for t in all_slots if t not in scalar_slots[step]])
-            for n, product in enumerate(products + [None]):
-                if n == inter_at[step]:
-                    interleave_scalar(unit - 1)
-                if n == group_at[step]:
-                    if step == 0:
-                        quantize_x(6)
-                        quantize_x(7)
-                        order_u_codes(1, 1)
-                    clip_in_place(unit, scalar_slots[step])
-                    quantize_unit(unit - 1)
-                    interleave_gpsimd(unit)
-                if product is None:
-                    continue
-                if product[0] == B:
-                    base(*product[1:])
-                else:
-                    task(*product)
+        base(1, 0)
+        base(1, 1)
+        interleave_scalar(2)
+        task(0, 0)
+        task(0, 1)
+        base(0, 4)
+        task(0, 2)
+        task(0, 3)
+        quantize_x(6)
+        quantize_x(7)
+        order_u_codes(1, 1)
+        sbuf_group(3, first_slots)
 
-        last = H * T - 1
-        halves = (slice(0, NH // 2), slice(NH // 2, NH))
-        interleave_scalar(UNITS - 1)
+        step_head(4, all_slots)
+        base(0, 5)
+        task(0, 4)
+        base(0, 6)
+        interleave_scalar(3)
+        task(0, 5)
+        sbuf_group(4, all_slots)
+        base(0, 7)
+
+        step_head(5, all_slots[1:])
+        interleave_scalar(4)
+        task(0, 6)
+        task(0, 7)
+        base(1, 2)
+        sbuf_group(5, all_slots[1:])
+        task(1, 0)
+        task(1, 1)
+
+        step_head(6, all_slots[1:])
+        interleave_scalar(5)
+        task(1, 2)
+        base(1, 3)
+        base(1, 4)
+        sbuf_group(6, all_slots[1:])
+        task(1, 3)
+        task(1, 4)
+
+        last_unit = UNITS - 1
+        step_head(last_unit, all_slots)
+        interleave_scalar(last_unit - 1)
+        task(2, 0)
+        task(2, 1)
+        sbuf_group(last_unit, all_slots)
+        base(1, 5)
+        task(2, 2)
+        base(1, 6)
+        task(2, 3)
+        interleave_scalar(last_unit)
         task(2, 4)
-        quantize_unit(UNITS - 1)
+        quantize_unit(last_unit)
         task(2, 5)
         task_beside_vector(1, 5)
         task(2, 6)
         task(2, 7)
         task_beside_vector(1, 6)
-        for m in range(MT - 2):
-            task(last, m)
-        base(H - 1, MT - 1)
+        task(3, 0)
+        task_beside_vector(3, 1)
+        for m in range(2, MT - 3):
+            task(3, m)
+        nc.sync.dma_start(out=out_view[1][:, NH:N], in_=acc[1][1][:])
+        task(3, MT - 3)
+        base(1, MT - 1)
+        halves = (slice(0, NH // 2), slice(NH // 2, NH))
         for cols in halves:
-            task(last, MT - 2, cols, slice(0, NH))
+            task(3, MT - 2, cols, slice(0, NH))
         for cols in halves:
             task(1, MT - 1, cols)
         for cols in (halves[0], slice(NH // 2, 3 * NH // 4), slice(3 * NH // 4, NH)):
-            task(last, MT - 1, cols)
+            task(3, MT - 1, cols)

@@ -29,7 +29,7 @@ UNITS = H * T * G
 EARLY = MT // 2
 FIRST_UNITS = H * G
 GP_COLS_WIDE = 384
-GP_COLS_STEP = 320
+GP_COLS_STEP = 288
 GP_COLS_LAST = NH // 2
 WARM_N = 256
 WARM_PASSES = 7
@@ -92,16 +92,16 @@ def tile_clipped_task_arithmetic_s4_kernel(
             nc.sync.dma_start(out=w_sb[h][:], in_=words[:, :, NH * h : NH * (h + 1)])
 
         ws_flat = ws_sb[:].rearrange("p h g n -> p (h g n)")
-        nc.vector.memset(ws_flat.bitcast(I32), 0)
         nc.vector.memset(vs_sb[:].bitcast(I32), 0)
         nc.vector.memset(us_raw[:].bitcast(I32), 0)
+        nc.vector.memset(ws_flat.bitcast(I32), 0)
         load_scale_rows(vs_sb, v_scales[0], (3,), nc.gpsimd)
         make_identity(nc, ident[:])
         nc.vector.quantize_mx(out=warm_q[:].bitcast(E4M3), scales=warm_s[:], in_=ws_flat.bitcast(BF16))
         load_v(0, 0)
         load_u(0)
+        load_scale_rows(us_raw, u_scales[0], (0, 2, 1, 3))
         load_scale_rows(vs_sb, v_scales[0], (0, 2))
-        load_scale_rows(us_raw, u_scales[0])
         load_scale_rows(vs_sb, v_scales[0], (1,))
         with nc.allow_non_contiguous_dma(reason="four limits a partition and row"):
             nc.sync.dma_start(out=lim_hi[:], in_=lim.rearrange("i (g p t) -> p (i g) t", g=G, t=PACK))
@@ -112,10 +112,10 @@ def tile_clipped_task_arithmetic_s4_kernel(
         load_w(0)
         load_x(2)
         load_x(3)
-        nc.sync.dma_start(out=lam_sb[:], in_=lam.rearrange("(p m) i -> p (m i)", m=MT))
-        load_u(1)
-        load_w(1)
         load_scale_rows(ws_sb[:, 1], ws_rows[:, 1])
+        load_w(1)
+        load_u(1)
+        nc.sync.dma_start(out=lam_sb[:], in_=lam.rearrange("(p m) i -> p (m i)", m=MT))
         load_v(1, 0)
         load_v(1, 1)
 
@@ -225,7 +225,7 @@ def tile_clipped_task_arithmetic_s4_kernel(
             words = x_sb[m // 2][:, m % 2, :].bitcast(F32)
             nc.scalar.copy(out=x_sorted[m][:], in_=words.rearrange("p (w u) -> p u w", u=2))
 
-        def turn_x(m):
+        def turn_x(m, on_vector=False):
             ps = psum.tile([P, G, 2, P], F32, name="ps")
             words = x_sb[m // 2][:, m % 2, :].bitcast(F32)
             for g in range(G):
@@ -234,7 +234,10 @@ def tile_clipped_task_arithmetic_s4_kernel(
                         nc.tensor.transpose(ps[:, g, u, :], x_sorted[m][:, u, P * g : P * (g + 1)], ident[:])
                     else:
                         nc.tensor.transpose(ps[:, g, u, :], words[:, 2 * P * g + u : 2 * P * (g + 1) : 2], ident[:])
-            nc.scalar.copy(out=xg[m][:].bitcast(F32), in_=ps[:].rearrange("p g u n -> p g n u"))
+            if on_vector:
+                nc.vector.tensor_copy(out=xg[m][:].bitcast(F32), in_=ps[:].rearrange("p g u n -> p g n u"))
+            else:
+                nc.scalar.copy(out=xg[m][:].bitcast(F32), in_=ps[:].rearrange("p g u n -> p g n u"))
 
         def quantize_x(m):
             nc.vector.quantize_mx(
@@ -307,10 +310,11 @@ def tile_clipped_task_arithmetic_s4_kernel(
         warm_up()
         for g in range(G):
             order_u_codes(0, g)
+        for g in range(G):
             order_u_scales(0, g)
-        negate_limits()
         for g in range(G):
             order_u_scales(1, g)
+        negate_limits()
         for j in range(FIRST_UNITS - 1):
             task_vectors(j)
             copy_out(j, first_slots)
@@ -321,7 +325,7 @@ def tile_clipped_task_arithmetic_s4_kernel(
         task_vectors(3, first_slots)
         copy_out(3, first_slots)
         for m in range(EARLY):
-            turn_x(m)
+            turn_x(m, m == 0)
         quantize_x(0)
         quantize_unit(0)
         quantize_x(1)
@@ -360,30 +364,30 @@ def tile_clipped_task_arithmetic_s4_kernel(
         order_u_codes(1, 1)
         sbuf_group(3, first_slots)
 
-        step_head(4, all_slots)
+        step_head(4, all_slots[:3])
         base(0, 5)
         task(0, 4)
         base(0, 6)
         interleave_scalar(3)
         task(0, 5)
-        sbuf_group(4, all_slots)
+        sbuf_group(4, all_slots[:3])
         base(0, 7)
 
-        step_head(5, all_slots[1:])
+        step_head(5, all_slots[:3])
         interleave_scalar(4)
         task(0, 6)
         task(0, 7)
         base(1, 2)
-        sbuf_group(5, all_slots[1:])
+        sbuf_group(5, all_slots[:3])
         task(1, 0)
         task(1, 1)
 
-        step_head(6, all_slots[1:])
+        step_head(6, all_slots[:3])
         interleave_scalar(5)
         task(1, 2)
         base(1, 3)
         base(1, 4)
-        sbuf_group(6, all_slots[1:])
+        sbuf_group(6, all_slots[:3])
         task(1, 3)
         task(1, 4)
 

@@ -31,8 +31,7 @@ FIRST_UNITS = H * G
 GP_COLS_WIDE = 384
 GP_COLS_STEP = 288
 GP_COLS_LAST = NH // 2
-WARM_N = 256
-WARM_PASSES = 7
+WARM_PASSES = 4
 
 
 def tile_clipped_task_arithmetic_s4_kernel(
@@ -61,8 +60,6 @@ def tile_clipped_task_arithmetic_s4_kernel(
         cq = [keep.tile([P, NH], U32, name=f"cq{j}", align_bytes=64) for j in range(UNITS)]
         cs = [keep.tile([P, NH], U8, name=f"cs{j}", align_bytes=64) for j in range(UNITS)]
         acc = [[keep.tile([P, NH], F32, name=f"acc{h}_{m}", align_bytes=64) for m in range(MT)] for h in range(H)]
-        warm_q = keep.tile([P, WARM_N], U32, name="warm_q", align_bytes=64)
-        warm_s = keep.tile([P, WARM_N], U8, name="warm_s", align_bytes=64)
         ident = keep.tile([P, P], F32, name="ident")
         lim_hi = keep.tile([P, T * G, PACK], BF16, name="lim_hi")
         lim_lo = keep.tile([P, T * G, PACK], BF16, name="lim_lo")
@@ -97,7 +94,17 @@ def tile_clipped_task_arithmetic_s4_kernel(
         nc.vector.memset(ws_flat.bitcast(I32), 0)
         load_scale_rows(vs_sb, v_scales[0], (3,), nc.gpsimd)
         make_identity(nc, ident[:])
-        nc.vector.quantize_mx(out=warm_q[:].bitcast(E4M3), scales=warm_s[:], in_=ws_flat.bitcast(BF16))
+        warm_ps = psum.tile([P, NH], F32, name="ps")
+        for r in range(WARM_PASSES):
+            nc.tensor.matmul_mx(
+                out=warm_ps[:],
+                lhsT=ws_flat[:, 0 : PACK * P].bitcast(E4M3),
+                lhsT_scale=ws_flat[:, 0:P],
+                rhs=ws_flat.bitcast(E4M3),
+                rhs_scale=ws_flat[:, 0:NH],
+                start=True,
+                stop=True,
+            )
         load_v(0, 0)
         load_u(0)
         load_scale_rows(us_raw, u_scales[0], (0, 2, 1, 3))
@@ -132,19 +139,6 @@ def tile_clipped_task_arithmetic_s4_kernel(
                 out=us_ord[i][g][:],
                 in_=us_raw[:, K * i + KP * g : K * i + KP * (g + 1)].rearrange("p (m t) -> p t m", t=PACK),
             )
-
-        def warm_up():
-            ps = psum.tile([P, NH], F32, name="ps")
-            for r in range(WARM_PASSES):
-                nc.tensor.matmul_mx(
-                    out=ps[:, 0:WARM_N],
-                    lhsT=warm_q[:, 0:P].bitcast(E4M3),
-                    lhsT_scale=warm_s[:, 0:P],
-                    rhs=warm_q[:].bitcast(E4M3),
-                    rhs_scale=warm_s[:],
-                    start=True,
-                    stop=True,
-                )
 
         def negate_limits():
             nc.vector.tensor_scalar(out=lim_lo[:], in0=lim_hi[:], scalar1=-1.0, scalar2=None, op0=ALU.mult)
@@ -307,7 +301,6 @@ def tile_clipped_task_arithmetic_s4_kernel(
         first_slots, last_slots, all_slots = (0, 1), (2, 3), tuple(range(PACK))
         late_tiles = range(EARLY, MT)
 
-        warm_up()
         for g in range(G):
             order_u_codes(0, g)
         for g in range(G):

@@ -54,7 +54,7 @@ def tile_clipped_task_arithmetic_s4_kernel(
         ws_sb = keep.tile([P, H, G, NH], U8, name="ws_sb", align_bytes=64)
         x_sb = [keep.tile([P, 2, K], BF16, name=f"x{c}", align_bytes=64) for c in range(MT // 2)]
         xg = [keep.tile([P, G, P, PACK], BF16, name=f"xg{m}", align_bytes=64) for m in range(MT)]
-        x_sorted = {m: keep.tile([P, 2, G * P], F32, name=f"x_sorted{m}", align_bytes=64) for m in range(EARLY, MT)}
+        x_sorted = {m: keep.tile([P, 2, G * P], F32, name=f"x_sorted{m}", align_bytes=64) for m in (4, 5, 6)}
         xq = [keep.tile([P, G, P], U32, name=f"xq{m}", align_bytes=64) for m in range(MT)]
         xs = [keep.tile([P, G, P], U8, name=f"xs{m}", align_bytes=64) for m in range(MT)]
         cq = [keep.tile([P, NH], U32, name=f"cq{j}", align_bytes=64) for j in range(UNITS)]
@@ -320,20 +320,21 @@ def tile_clipped_task_arithmetic_s4_kernel(
         for m in range(EARLY):
             turn_x(m, m == 0)
         quantize_x(0)
-        quantize_unit(0)
         quantize_x(1)
+        quantize_unit(0)
         quantize_x(2)
         quantize_x(3)
         clip_in_place(1, first_slots)
         interleave_gpsimd(1)
         task_vectors(3, last_slots)
         clip_out(3, last_slots)
-        for m in late_tiles:
+        for m in x_sorted:
             sort_x(m)
         interleave_scalar(1)
-        for m in range(EARLY - 1):
+        for m in range(2):
             base_on_vector(0, m)
-        base(0, EARLY - 1)
+        base(0, 2)
+        base(0, 3)
         for m in late_tiles:
             turn_x(m)
         quantize_unit(1)

@@ -29,7 +29,7 @@ UNITS = H * T * G
 EARLY = MT // 2
 FIRST_UNITS = H * G
 GP_COLS_WIDE = 384
-GP_COLS_STEP = 288
+GP_COLS_STEP = 320
 GP_COLS_LAST = NH // 2
 WARM_PASSES = 4
 
@@ -129,6 +129,12 @@ def tile_clipped_task_arithmetic_s4_kernel(
         units = [(h, i, g) for i in range(T) for h in range(H) for g in range(G)]
 
         def order_u_codes(i, g):
+            nc.scalar.copy(
+                out=u_ord[i][g][:].bitcast(U16),
+                in_=u_raw[i][:, 2 * KP * g : 2 * KP * (g + 1)].bitcast(U16).rearrange("p (m t) -> p t m", t=PACK),
+            )
+
+        def order_u_codes_vector(i, g):
             nc.vector.tensor_copy(
                 out=u_ord[i][g][:].bitcast(U16),
                 in_=u_raw[i][:, 2 * KP * g : 2 * KP * (g + 1)].bitcast(U16).rearrange("p (m t) -> p t m", t=PACK),
@@ -281,12 +287,13 @@ def tile_clipped_task_arithmetic_s4_kernel(
                 stored = stored or cols
                 nc.sync.dma_start(out=out_view[m][:, NH * h + stored.start : NH * h + stored.stop], in_=acc[h][m][:, stored])
 
-        def task_beside_vector(pair, m):
+        def task_beside_vector(pair, m, total=None):
             i, h = divmod(pair, H)
             ps = task_product(pair, m, slice(0, NH))
             part = work.tile([P, NH], F32, name="part", align_bytes=64)
             nc.scalar.activation(out=part[:], in_=ps[:], func=ACT.Copy, scale=lam_f[:, m * T + i : m * T + i + 1])
-            nc.gpsimd.tensor_tensor(out=acc[h][m][:], in0=acc[h][m][:], in1=part[:], op=ALU.add)
+            total = acc[h][m] if total is None else total
+            nc.gpsimd.tensor_tensor(out=total[:], in0=acc[h][m][:], in1=part[:], op=ALU.add)
 
         def sbuf_group(unit, slots):
             clip_in_place(unit, slots)
@@ -299,21 +306,22 @@ def tile_clipped_task_arithmetic_s4_kernel(
             clip_out(unit, [t for t in all_slots if t not in scalar_slots])
 
         first_slots, last_slots, all_slots = (0, 1), (2, 3), tuple(range(PACK))
+        even_slots, odd_slots = all_slots[0::2], all_slots[1::2]
         late_tiles = range(EARLY, MT)
 
-        for g in range(G):
-            order_u_codes(0, g)
+        order_u_codes_vector(0, 0)
+        order_u_codes(0, 1)
         for g in range(G):
             order_u_scales(0, g)
-        for g in range(G):
-            order_u_scales(1, g)
+        order_u_scales(1, 0)
         negate_limits()
+        order_u_scales(1, 1)
         for j in range(FIRST_UNITS - 1):
             task_vectors(j)
-            copy_out(j, first_slots)
-            clip_out(j, last_slots)
+            copy_out(j, even_slots)
+            clip_out(j, odd_slots)
             if j == 0:
-                clip_in_place(0, first_slots)
+                clip_in_place(0, even_slots)
                 interleave_gpsimd(0)
         task_vectors(3, first_slots)
         copy_out(3, first_slots)
@@ -324,7 +332,7 @@ def tile_clipped_task_arithmetic_s4_kernel(
         quantize_unit(0)
         quantize_x(2)
         quantize_x(3)
-        clip_in_place(1, first_slots)
+        clip_in_place(1, even_slots)
         interleave_gpsimd(1)
         task_vectors(3, last_slots)
         clip_out(3, last_slots)
@@ -340,8 +348,8 @@ def tile_clipped_task_arithmetic_s4_kernel(
         quantize_unit(1)
         quantize_x(4)
         quantize_x(5)
-        order_u_codes(1, 0)
-        clip_in_place(2, first_slots)
+        order_u_codes_vector(1, 0)
+        clip_in_place(2, even_slots)
         interleave_gpsimd(2)
         nc.scalar.copy(out=lam_f[:], in_=lam_sb[:])
 
@@ -351,11 +359,11 @@ def tile_clipped_task_arithmetic_s4_kernel(
         task(0, 0)
         task(0, 1)
         base(0, 4)
+        order_u_codes(1, 1)
         task(0, 2)
         task(0, 3)
         quantize_x(6)
         quantize_x(7)
-        order_u_codes(1, 1)
         sbuf_group(3, first_slots)
 
         step_head(4, all_slots[:3])
@@ -398,22 +406,25 @@ def tile_clipped_task_arithmetic_s4_kernel(
         interleave_scalar(last_unit)
         task(2, 4)
         quantize_unit(last_unit)
-        task(2, 5)
-        task_beside_vector(1, 5)
+        halves = (slice(0, NH // 2), slice(NH // 2, NH))
+        total = keep.tile([P, NH], F32, name="grp", align_bytes=64)
+        task_beside_vector(2, 5, total)
         task(2, 6)
+        task_beside_vector(1, 5)
         task(2, 7)
+        nc.sync.dma_start(out=out_view[5][:, NH * 0 : NH * (0 + 1)], in_=total[:])
         task_beside_vector(1, 6)
         task(3, 0)
-        task_beside_vector(3, 1)
-        for m in range(2, MT - 3):
-            task(3, m)
-        nc.sync.dma_start(out=out_view[1][:, NH:N], in_=acc[1][1][:])
-        task(3, MT - 3)
-        base(1, MT - 1)
-        halves = (slice(0, NH // 2), slice(NH // 2, NH))
+        task(3, 1)
+        task(3, 2)
+        task_beside_vector(3, 3)
+        task(3, 4)
+        task(3, 5)
+        base(1, 7)
+        nc.sync.dma_start(out=out_view[3][:, NH * 1 : NH * (1 + 1)], in_=acc[1][3][:])
         for cols in halves:
-            task(3, MT - 2, cols, slice(0, NH))
+            task(3, 6, cols, slice(0, NH))
         for cols in halves:
-            task(1, MT - 1, cols)
+            task(1, 7, cols)
         for cols in (halves[0], slice(NH // 2, 3 * NH // 4), slice(3 * NH // 4, NH)):
-            task(3, MT - 1, cols)
+            task(3, 7, cols)

from contextlib import ExitStack

import concourse.mybir as mybir
from concourse.masks import make_identity

M, K, N, R, T = 1024, 1024, 1024, 512, 2

F32 = mybir.dt.float32
BF16 = mybir.dt.bfloat16
I32 = mybir.dt.int32
U32 = mybir.dt.uint32
U16 = mybir.dt.uint16
U8 = mybir.dt.uint8
E4M3 = mybir.dt.float8_e4m3fn_x4
E2M1 = mybir.dt.float4_e2m1fn_x4
ALU = mybir.AluOpType
ACT = mybir.ActivationFunctionType

FLOPS = 2 * M * K * N * (1 + T) + 2 * T * R * K * N

P = 128
PACK = 4
KP = P * PACK
NH = 512
MT = M // P
G = K // KP
H = N // NH
UNITS = H * T * G
EARLY = MT // 2
FIRST_UNITS = H * G
GP_COLS_WIDE = 384
GP_COLS_STEP = 320
GP_COLS_LAST = NH // 2
WARM_PASSES = 4


def tile_clipped_task_arithmetic_s4_kernel(
    tc, x, w_words, w_scales, u_words, u_scales, v_words, v_scales, lim, lam, out
):
    nc = tc.nc
    with ExitStack() as ctx:
        keep = ctx.enter_context(tc.tile_pool(name="keep", bufs=1))
        work = ctx.enter_context(tc.tile_pool(name="work", bufs=4))
        psum = ctx.enter_context(tc.psum_pool(name="psum", bufs=8))
        ctx.enter_context(tc.manual_schedule())

        u_raw = [keep.tile([P, 2 * K], U8, name=f"u_raw{i}", align_bytes=64) for i in range(T)]
        u_ord = [[keep.tile([P, PACK, 2 * P], U8, name=f"u_ord{i}_{g}", align_bytes=64) for g in range(G)] for i in range(T)]
        us_raw = keep.tile([P, T * K], U8, name="us_raw", align_bytes=64)
        us_ord = [[keep.tile([P, PACK, P], U8, name=f"us_ord{i}_{g}", align_bytes=64) for g in range(G)] for i in range(T)]
        v_sb = [[keep.tile([P, 2 * NH], U8, name=f"v{i}_{h}", align_bytes=64) for h in range(H)] for i in range(T)]
        vs_sb = keep.tile([P, T * N], U8, name="vs_sb", align_bytes=64)
        w_sb = [keep.tile([P, G, NH], I32, name=f"w{h}", align_bytes=64) for h in range(H)]
        ws_sb = keep.tile([P, H, G, NH], U8, name="ws_sb", align_bytes=64)
        x_sb = [keep.tile([P, 2, K], BF16, name=f"x{c}", align_bytes=64) for c in range(MT // 2)]
        xg = [keep.tile([P, G, P, PACK], BF16, name=f"xg{m}", align_bytes=64) for m in range(MT)]
        x_sorted = {m: keep.tile([P, 2, G * P], F32, name=f"x_sorted{m}", align_bytes=64) for m in (4, 5, 6)}
        xq = [keep.tile([P, G, P], U32, name=f"xq{m}", align_bytes=64) for m in range(MT)]
        xs = [keep.tile([P, G, P], U8, name=f"xs{m}", align_bytes=64) for m in range(MT)]
        cq = [keep.tile([P, NH], U32, name=f"cq{j}", align_bytes=64) for j in range(UNITS)]
        cs = [keep.tile([P, NH], U8, name=f"cs{j}", align_bytes=64) for j in range(UNITS)]
        acc = [[keep.tile([P, NH], F32, name=f"acc{h}_{m}", align_bytes=64) for m in range(MT)] for h in range(H)]
        ident = keep.tile([P, P], F32, name="ident")
        lim_hi = keep.tile([P, T * G, PACK], BF16, name="lim_hi")
        lim_lo = keep.tile([P, T * G, PACK], BF16, name="lim_lo")
        lam_sb = keep.tile([P, MT * T], BF16, name="lam_sb")
        lam_f = keep.tile([P, MT * T], F32, name="lam_f")

        x_view = x.rearrange("(p m) k -> p m k", m=MT)
        out_view = out.rearrange("(p m) n -> m p n", m=MT)
        ws_rows = w_scales.rearrange("g r (h n) -> r h g n", h=H)

        def load_u(i):
            nc.sync.dma_start(out=u_raw[i][:].bitcast(I32), in_=u_words[0, :, 2 * K * i : 2 * K * (i + 1)].bitcast(I32))

        def load_v(i, h):
            c0 = 2 * (N * i + NH * h)
            nc.sync.dma_start(out=v_sb[i][h][:].bitcast(I32), in_=v_words[0, :, c0 : c0 + 2 * NH].bitcast(I32))

        def load_scale_rows(plane, rows, quadrants=range(4), queue=nc.sync):
            for q in quadrants:
                queue.dma_start(out=plane[32 * q : 32 * q + 4].bitcast(I32), in_=rows[4 * q : 4 * q + 4].bitcast(I32))

        def load_x(c):
            nc.sync.dma_start(out=x_sb[c][:], in_=x_view[:, 2 * c : 2 * c + 2, :])

        def load_w(h):
            words = w_words.rearrange("g p n t -> p g (n t)").bitcast(I32)
            nc.sync.dma_start(out=w_sb[h][:], in_=words[:, :, NH * h : NH * (h + 1)])

        ws_flat = ws_sb[:].rearrange("p h g n -> p (h g n)")
        nc.vector.memset(vs_sb[:].bitcast(I32), 0)
        nc.vector.memset(us_raw[:].bitcast(I32), 0)
        nc.vector.memset(ws_flat.bitcast(I32), 0)
        load_scale_rows(vs_sb, v_scales[0], (3,), nc.gpsimd)
        make_identity(nc, ident[:])
        warm_ps = psum.tile([P, NH], F32, name="ps")
        for r in range(WARM_PASSES):
            nc.tensor.matmul_mx(
                out=warm_ps[:],
                lhsT=ws_flat[:, 0 : PACK * P].bitcast(E4M3),
                lhsT_scale=ws_flat[:, 0:P],
                rhs=ws_flat.bitcast(E4M3),
                rhs_scale=ws_flat[:, 0:NH],
                start=True,
                stop=True,
            )
        load_v(0, 0)
        load_u(0)
        load_scale_rows(us_raw, u_scales[0], (0, 2, 1, 3))
        load_scale_rows(vs_sb, v_scales[0], (0, 2))
        load_scale_rows(vs_sb, v_scales[0], (1,))
        with nc.allow_non_contiguous_dma(reason="four limits a partition and row"):
            nc.sync.dma_start(out=lim_hi[:], in_=lim.rearrange("i (g p t) -> p (i g) t", g=G, t=PACK))
        load_v(0, 1)
        load_x(0)
        load_x(1)
        load_scale_rows(ws_sb[:, 0], ws_rows[:, 0])
        load_w(0)
        load_x(2)
        load_x(3)
        load_scale_rows(ws_sb[:, 1], ws_rows[:, 1])
        load_w(1)
        load_u(1)
        nc.sync.dma_start(out=lam_sb[:], in_=lam.rearrange("(p m) i -> p (m i)", m=MT))
        load_v(1, 0)
        load_v(1, 1)

        units = [(h, i, g) for i in range(T) for h in range(H) for g in range(G)]

        def order_u_codes(i, g):
            nc.scalar.copy(
                out=u_ord[i][g][:].bitcast(U16),
                in_=u_raw[i][:, 2 * KP * g : 2 * KP * (g + 1)].bitcast(U16).rearrange("p (m t) -> p t m", t=PACK),
            )

        def order_u_codes_vector(i, g):
            nc.vector.tensor_copy(
                out=u_ord[i][g][:].bitcast(U16),
                in_=u_raw[i][:, 2 * KP * g : 2 * KP * (g + 1)].bitcast(U16).rearrange("p (m t) -> p t m", t=PACK),
            )

        def order_u_scales(i, g):
            nc.vector.tensor_copy(
                out=us_ord[i][g][:],
                in_=us_raw[:, K * i + KP * g : K * i + KP * (g + 1)].rearrange("p (m t) -> p t m", t=PACK),
            )

        def negate_limits():
            nc.vector.tensor_scalar(out=lim_lo[:], in0=lim_hi[:], scalar1=-1.0, scalar2=None, op0=ALU.mult)

        d_ps = {}
        d_sb = {}
        grp = {}

        def task_vectors(j, slots=range(PACK)):
            h, i, g = units[j]
            if j not in d_sb:
                d_sb[j] = work.tile([P, PACK, NH], BF16, name="d_sb", align_bytes=64)
            for t in slots:
                d_ps[j, t] = psum.tile([P, NH], F32, name="ps")
                nc.tensor.matmul_mx(
                    out=d_ps[j, t][:],
                    lhsT=u_ord[i][g][:, t, :].bitcast(E2M1),
                    lhsT_scale=us_ord[i][g][:, t, :],
                    rhs=v_sb[i][h][:].bitcast(E2M1),
                    rhs_scale=vs_sb[:, N * i + NH * h : N * i + NH * (h + 1)],
                    start=True,
                    stop=True,
                )

        def clip(j, t, src):
            h, i, g = units[j]
            nc.vector.tensor_scalar(
                out=d_sb[j][:, t, :],
                in0=src,
                scalar1=lim_hi[:, i * G + g, t : t + 1],
                scalar2=lim_lo[:, i * G + g, t : t + 1],
                op0=ALU.min,
                op1=ALU.max,
            )

        def copy_out(j, slots):
            for t in slots:
                nc.scalar.copy(out=d_sb[j][:, t, :], in_=d_ps[j, t][:])

        def clip_in_place(j, slots):
            for t in slots:
                clip(j, t, d_sb[j][:, t, :])

        def clip_out(j, slots):
            for t in slots:
                clip(j, t, d_ps[j, t][:])

        def gpsimd_cols(j):
            if j == 0:
                return NH
            if j == UNITS - 1:
                return GP_COLS_LAST
            return GP_COLS_STEP if FIRST_UNITS - 1 <= j < UNITS - 2 else GP_COLS_WIDE

        def interleave_gpsimd(j):
            cols = gpsimd_cols(j)
            grp[j] = keep.tile([P, NH, PACK], BF16, name="grp", align_bytes=64)
            nc.gpsimd.tensor_scalar(
                out=grp[j][:, 0:cols, :],
                in0=d_sb[j][:, :, 0:cols].rearrange("p t n -> p n t"),
                scalar1=1.0,
                scalar2=0.0,
                op0=ALU.mult,
                op1=ALU.add,
            )

        def interleave_scalar(j):
            cols = gpsimd_cols(j)
            nc.scalar.copy(
                out=grp[j][:, cols:NH, :].rearrange("p (c i) t -> p c t i", i=4),
                in_=d_sb[j][:, :, cols:NH].rearrange("p t (c i) -> p c t i", i=4),
            )

        def quantize_unit(j):
            nc.vector.quantize_mx(out=cq[j][:].bitcast(E4M3), scales=cs[j][:], in_=grp[j][:].rearrange("p n t -> p (n t)"))

        def sort_x(m):
            words = x_sb[m // 2][:, m % 2, :].bitcast(F32)
            nc.scalar.copy(out=x_sorted[m][:], in_=words.rearrange("p (w u) -> p u w", u=2))

        def turn_x(m, on_vector=False):
            ps = psum.tile([P, G, 2, P], F32, name="ps")
            words = x_sb[m // 2][:, m % 2, :].bitcast(F32)
            for g in range(G):
                for u in range(2):
                    if m in x_sorted:
                        nc.tensor.transpose(ps[:, g, u, :], x_sorted[m][:, u, P * g : P * (g + 1)], ident[:])
                    else:
                        nc.tensor.transpose(ps[:, g, u, :], words[:, 2 * P * g + u : 2 * P * (g + 1) : 2], ident[:])
            if on_vector:
                nc.vector.tensor_copy(out=xg[m][:].bitcast(F32), in_=ps[:].rearrange("p g u n -> p g n u"))
            else:
                nc.scalar.copy(out=xg[m][:].bitcast(F32), in_=ps[:].rearrange("p g u n -> p g n u"))

        def quantize_x(m):
            nc.vector.quantize_mx(
                out=xq[m][:].rearrange("p g n -> p (g n)").bitcast(E4M3),
                scales=xs[m][:].rearrange("p g n -> p (g n)"),
                in_=xg[m][:].rearrange("p g n t -> p (g n t)"),
            )

        def x_times(m, codes, scales, cols):
            ps = psum.tile([P, NH], F32, name="ps")
            for g in range(G):
                nc.tensor.matmul_mx(
                    out=ps[:, cols],
                    lhsT=xq[m][:, g, :].bitcast(E4M3),
                    lhsT_scale=xs[m][:, g, :],
                    rhs=codes[g][:, cols].bitcast(E4M3),
                    rhs_scale=scales[g][:, cols],
                    start=(g == 0),
                    stop=(g == G - 1),
                )
            return ps

        def base_product(h, m):
            return x_times(m, [w_sb[h][:, g, :] for g in range(G)], [ws_sb[:, h, g, :] for g in range(G)], slice(0, NH))

        def base(h, m):
            nc.scalar.copy(out=acc[h][m][:], in_=base_product(h, m)[:])

        def base_on_vector(h, m):
            nc.vector.tensor_copy(out=acc[h][m][:], in_=base_product(h, m)[:])

        def task_product(pair, m, cols):
            return x_times(m, cq[G * pair : G * (pair + 1)], cs[G * pair : G * (pair + 1)], cols)

        def task(pair, m, cols=slice(0, NH), stored=None):
            i, h = divmod(pair, H)
            ps = task_product(pair, m, cols)
            nc.vector.scalar_tensor_tensor(
                out=acc[h][m][:, cols],
                in0=ps[:, cols],
                scalar=lam_sb[:, m * T + i : m * T + i + 1],
                in1=acc[h][m][:, cols],
                op0=ALU.mult,
                op1=ALU.add,
            )
            if i == T - 1 and (stored is None or stored.stop == cols.stop):
                stored = stored or cols
                nc.sync.dma_start(out=out_view[m][:, NH * h + stored.start : NH * h + stored.stop], in_=acc[h][m][:, stored])

        def task_beside_vector(pair, m, total=None):
            i, h = divmod(pair, H)
            ps = task_product(pair, m, slice(0, NH))
            part = work.tile([P, NH], F32, name="part", align_bytes=64)
            nc.scalar.activation(out=part[:], in_=ps[:], func=ACT.Copy, scale=lam_f[:, m * T + i : m * T + i + 1])
            total = acc[h][m] if total is None else total
            nc.gpsimd.tensor_tensor(out=total[:], in0=acc[h][m][:], in1=part[:], op=ALU.add)

        def sbuf_group(unit, slots):
            clip_in_place(unit, slots)
            quantize_unit(unit - 1)
            interleave_gpsimd(unit)

        def step_head(unit, scalar_slots):
            task_vectors(unit)
            copy_out(unit, scalar_slots)
            clip_out(unit, [t for t in all_slots if t not in scalar_slots])

        first_slots, last_slots, all_slots = (0, 1), (2, 3), tuple(range(PACK))
        even_slots, odd_slots = all_slots[0::2], all_slots[1::2]
        late_tiles = range(EARLY, MT)

        order_u_codes_vector(0, 0)
        order_u_codes(0, 1)
        for g in range(G):
            order_u_scales(0, g)
        order_u_scales(1, 0)
        negate_limits()
        order_u_scales(1, 1)
        for j in range(FIRST_UNITS - 1):
            task_vectors(j)
            copy_out(j, even_slots)
            clip_out(j, odd_slots)
            if j == 0:
                clip_in_place(0, even_slots)
                interleave_gpsimd(0)
        task_vectors(3, first_slots)
        copy_out(3, first_slots)
        for m in range(EARLY):
            turn_x(m, m == 0)
        quantize_x(0)
        quantize_x(1)
        quantize_unit(0)
        quantize_x(2)
        quantize_x(3)
        clip_in_place(1, even_slots)
        interleave_gpsimd(1)
        task_vectors(3, last_slots)
        clip_out(3, last_slots)
        for m in x_sorted:
            sort_x(m)
        interleave_scalar(1)
        for m in range(2):
            base_on_vector(0, m)
        base(0, 2)
        base(0, 3)
        for m in late_tiles:
            turn_x(m)
        quantize_unit(1)
        quantize_x(4)
        quantize_x(5)
        order_u_codes_vector(1, 0)
        clip_in_place(2, even_slots)
        interleave_gpsimd(2)
        nc.scalar.copy(out=lam_f[:], in_=lam_sb[:])

        base(1, 0)
        base(1, 1)
        interleave_scalar(2)
        task(0, 0)
        task(0, 1)
        base(0, 4)
        order_u_codes(1, 1)
        task(0, 2)
        task(0, 3)
        quantize_x(6)
        quantize_x(7)
        sbuf_group(3, first_slots)

        step_head(4, all_slots[:3])
        base(0, 5)
        task(0, 4)
        base(0, 6)
        interleave_scalar(3)
        task(0, 5)
        sbuf_group(4, all_slots[:3])
        base(0, 7)

        step_head(5, all_slots[:3])
        interleave_scalar(4)
        task(0, 6)
        task(0, 7)
        base(1, 2)
        sbuf_group(5, all_slots[:3])
        task(1, 0)
        task(1, 1)

        step_head(6, all_slots[:3])
        interleave_scalar(5)
        task(1, 2)
        base(1, 3)
        base(1, 4)
        sbuf_group(6, all_slots[:3])
        task(1, 3)
        task(1, 4)

        last_unit = UNITS - 1
        step_head(last_unit, all_slots)
        interleave_scalar(last_unit - 1)
        task(2, 0)
        task(2, 1)
        sbuf_group(last_unit, all_slots)
        base(1, 5)
        task(2, 2)
        base(1, 6)
        task(2, 3)
        interleave_scalar(last_unit)
        task(2, 4)
        quantize_unit(last_unit)
        halves = (slice(0, NH // 2), slice(NH // 2, NH))
        total = keep.tile([P, NH], F32, name="grp", align_bytes=64)
        task_beside_vector(2, 5, total)
        task(2, 6)
        task_beside_vector(1, 5)
        task(2, 7)
        nc.sync.dma_start(out=out_view[5][:, NH * 0 : NH * (0 + 1)], in_=total[:])
        task_beside_vector(1, 6)
        task(3, 0)
        task(3, 1)
        task(3, 2)
        task_beside_vector(3, 3)
        task(3, 4)
        task(3, 5)
        base(1, 7)
        nc.sync.dma_start(out=out_view[3][:, NH * 1 : NH * (1 + 1)], in_=acc[1][3][:])
        for cols in halves:
            task(3, 6, cols, slice(0, NH))
        for cols in halves:
            task(1, 7, cols)
        for cols in (halves[0], slice(NH // 2, 3 * NH // 4), slice(3 * NH // 4, NH)):
            task(3, 7, cols)
